import numpy as np
import ml_dtypes


def mxq(x, axis, fmt="e4m3"):
    dtype, down = {"e4m3": (ml_dtypes.float8_e4m3fn, 7), "e5m2": (ml_dtypes.float8_e5m2, 14)}[fmt]
    v = np.moveaxis(np.asarray(x, np.float32).astype(ml_dtypes.bfloat16).astype(np.float64), axis, -1)
    blocks = v.reshape(v.shape[:-1] + (-1, 32))
    amax = np.abs(blocks).max(-1, keepdims=True)
    byte = np.maximum(np.where(amax > 0, np.frexp(amax)[1] - 1 + 127, 0) - down, 1)
    scale = np.exp2(byte - 127.0)
    codes = (blocks / scale).astype(np.float32).astype(dtype).astype(np.float64)
    return np.moveaxis((codes * scale).reshape(v.shape), -1, axis)


WIDE = False


def mx_kscale(k):
    if not WIDE:
        return np.ones(k)
    levels = np.array([10, -10, 5, -5, 0])
    if k % 512:
        return np.exp2(np.random.permutation(np.resize(levels, k // 32))).repeat(32)
    a = np.empty((k // 512, 16))
    for p in range(k // 512):
        a[p, :8] = np.random.permutation(np.resize(levels, 8))
        for g in range(8):
            far = levels[np.abs(levels - a[p, g]) >= 10]
            a[p, g + 8] = far[np.random.randint(len(far))]
    return np.exp2(a.ravel()).repeat(32)


def f64(x):
    return np.asarray(x).astype(np.float64)


def striped(idx):
    return np.tile(idx.reshape(-1, 16).T, (8, 1)).astype(np.uint16)


def unstriped(offs):
    return offs[:16].T.reshape(-1).astype(np.int64)


def pack_weight(w):
    k, n = w.shape
    w = f64(np.asarray(w, np.float32).astype(ml_dtypes.bfloat16)).reshape(k // 32, 32, n)
    amax = np.abs(w).max(1)
    byte = np.clip(np.where(amax > 0, np.frexp(amax)[1] - 1 + 127 - 7, 1), 1, 254)
    scaled = (w * np.exp2(127.0 - byte)[:, None, :]).reshape(k, n).astype(np.float32)
    words = np.ascontiguousarray(scaled.reshape(k // 512, 128, 4, n).transpose(0, 1, 3, 2)).astype(ml_dtypes.float8_e4m3fn).view(np.uint8)
    return words, np.ascontiguousarray(byte.astype(np.uint8).reshape(k // 512, 16, n))


def unpack_weight(words, scales):
    g, p, n, _ = words.shape
    vals = np.ascontiguousarray(words).view(ml_dtypes.float8_e4m3fn).astype(np.float64) * np.repeat(np.exp2(scales.astype(np.float64) - 127.0), 8, axis=1)[..., None]
    return vals.transpose(0, 1, 3, 2).reshape(g * 512, n)


E2M1 = np.array([0.0, 0.5, 1.0, 1.5, 2.0, 3.0, 4.0, 6.0, -0.0, -0.5, -1.0, -1.5, -2.0, -3.0, -4.0, -6.0])


def pack_fp4(w):
    k, n = w.shape
    w = f64(np.asarray(w, np.float32).astype(ml_dtypes.bfloat16)).reshape(k // 32, 32, n)
    amax = np.abs(w).max(1)
    mant, ex = np.frexp(amax / 6.0)
    byte = np.clip(np.where(amax > 0, np.where(mant > 0.5, ex, ex - 1) + 127, 1), 1, 254)
    scaled = (w * np.exp2(127.0 - byte)[:, None, :]).reshape(k, n).astype(np.float32)
    c = np.ascontiguousarray(scaled.reshape(k // 512, 128, 4, n).transpose(0, 1, 3, 2)).astype(ml_dtypes.float4_e2m1fn).view(np.uint8) & 0xF
    words = (c[..., 0::2] | (c[..., 1::2] << 4)).reshape(k // 512, 128, 2 * n)
    return np.ascontiguousarray(words), np.ascontiguousarray(byte.astype(np.uint8).reshape(k // 512, 16, n))


def unpack_fp4(words, scales):
    g, _, n = scales.shape
    words = np.ascontiguousarray(words).reshape(g, 128, n, 2)
    nib = np.empty((g, 128, n, 4), np.uint8)
    nib[..., 0::2] = words & 0xF
    nib[..., 1::2] = words >> 4
    vals = E2M1[nib] * np.repeat(np.exp2(scales.astype(np.float64) - 127.0), 8, axis=1)[..., None]
    return vals.transpose(0, 1, 3, 2).reshape(g * 512, n)


def planes(y):
    n, m = y.shape
    v = y.astype(np.float32).astype(ml_dtypes.bfloat16).astype(np.float64).reshape(n // 32, 32, m)
    top = np.abs(v).max(1)
    byte = np.clip(np.where(top > 0, np.frexp(top)[1] - 1 + 127 - 7, 1), 1, 254)
    codes = (v * np.exp2(127.0 - byte)[:, None, :]).reshape(n, m).astype(np.float32).astype(ml_dtypes.float8_e4m3fn).view(np.uint8)
    words = codes.reshape(n // 512, 128, 4, m).transpose(0, 1, 3, 2)
    return np.ascontiguousarray(words), np.ascontiguousarray(byte.astype(np.uint8).reshape(n // 512, 16, m))


def relu(v):
    return np.maximum(v, 0.0)


K, T, S, V, H, N = 1024, 1024, 512, 256, 512, 512


def setup_inputs():
    n = np.random.standard_normal
    s = mx_kscale(K)[:, None]
    u = mx_kscale(H)
    near = np.random.permutation(S)
    packed_xT = pack_weight(n((K, T)) * s)
    packed_w2 = pack_fp4(n((H, N)) / np.sqrt(H) / u[:, None])
    packed_w3 = pack_fp4(n((H, N)) / np.sqrt(H) / u[:, None])
    return {
        "x_words": packed_xT[0],
        "x_scales": packed_xT[1],
        "w1": (n((K, H)) / np.sqrt(K) / s * u).astype(np.float32),
        "w2_words": packed_w2[0],
        "w2_scales": packed_w2[1],
        "w3_words": packed_w3[0],
        "w3_scales": packed_w3[1],
        "offs": striped(np.random.permutation(T)[:S]),
        "pos1": striped(near[:V]),
        "pos2": striped(near[V:]),
    }


def reference(x_words, x_scales, w1, w2_words, w2_scales, w3_words, w3_scales, offs, pos1, pos2):
    xq = unpack_weight(x_words, x_scales)[:, unstriped(offs)]
    h = relu(mxq(f64(w1), 0, "e4m3").T @ xq)
    hq = mxq(h, 0, "e4m3")
    y = unpack_fp4(w3_words, w3_scales).T @ hq
    e = np.exp(unpack_fp4(w2_words, w2_scales).T @ hq)
    e0 = e[:, unstriped(pos1)]
    e1 = e[:, unstriped(pos2)]
    num = y[:, unstriped(pos1)] * e0 + y[:, unstriped(pos2)] * e1
    den = e0 + e1
    out_0 = num / den
    return (out_0,) + planes(out_0)

@@ -1,0 +1,289 @@
+from contextlib import ExitStack
+
+import concourse.mybir as mybir
+
+K, T, S, V, H, N = 1024, 1024, 512, 256, 512, 512
+FLOPS = 2 * S * (K * H + 2 * H * N)
+
+F32 = mybir.dt.float32
+BF16 = mybir.dt.bfloat16
+I32 = mybir.dt.int32
+U32 = mybir.dt.uint32
+U16 = mybir.dt.uint16
+U8 = mybir.dt.uint8
+FP8X4 = mybir.dt.float8_e4m3fn_x4
+FP4X4 = mybir.dt.float4_e2m1fn_x4
+ACT = mybir.ActivationFunctionType
+ALU = mybir.AluOpType
+
+P = 128
+PACK = 4
+PASSES = K // (P * PACK)
+BLOCK = 128
+BLOCKS = S // BLOCK
+HALF = H // 2
+
+
+def tile_picked_zrandla_relu_po_kernel(
+    tc, x_words, x_scales, w1, w2_words, w2_scales, w3_words, w3_scales, offs, pos1, pos2, out_0, out_1, out_2
+):
+    nc = tc.nc
+    with ExitStack() as ctx:
+        lists = ctx.enter_context(tc.tile_pool(name="lists", bufs=1))
+        keep = ctx.enter_context(tc.tile_pool(name="keep", bufs=1))
+        hidden_psum = ctx.enter_context(tc.psum_pool(name="hidden_psum", bufs=1))
+        head_psum = ctx.enter_context(tc.psum_pool(name="head_psum", bufs=4))
+
+        head_words = [keep.tile([P, 2 * N], U8, name=f"head_words{w}", align_bytes=64) for w in range(2)]
+        x_scale_rows = keep.tile([P, T], U8, align_bytes=64)
+        nc.gpsimd.memset(x_scale_rows[:].bitcast(I32), 0)
+        warm = keep.tile([P, 2], F32)
+        nc.gpsimd.memset(warm[:, 0:1], 0.0)
+        nc.scalar.activation(out=warm[:, 1:2], in_=warm[:, 0:1], func=ACT.Sigmoid)
+        head_scale_rows = [keep.tile([P, N], U8, name=f"head_scale_rows{w}", align_bytes=64) for w in range(2)]
+        for w in range(2):
+            nc.gpsimd.memset(head_scale_rows[w][:].bitcast(I32), 0)
+
+        w1_first = keep.tile([P, PACK, H], F32)
+        w1_second = [keep.tile([P, PACK, HALF], F32, name=f"w1_second{u}") for u in range(2)]
+        w1_raw = [[w1_first[:, :, u * HALF : (u + 1) * HALF] for u in range(2)], [w1_second[u][:] for u in range(2)]]
+        w1_rows = w1.rearrange("(g p j) c -> g p j c", p=P, j=PACK)
+        x_window = [keep.tile([P, T], I32, name=f"x_window{g}", align_bytes=64) for g in range(PASSES)]
+        x_scale_landing = keep.tile([P, T // 4], I32)
+        offs_t = lists.tile([P, S // 16], U16)
+        pos1_t = lists.tile([P, V // 16], U16)
+        pos2_t = lists.tile([P, V // 16], U16)
+
+        for w, words in enumerate((w2_words, w3_words)):
+            nc.sync.dma_start(out=head_words[w][:].bitcast(I32), in_=words[0].bitcast(I32))
+        nc.sync.dma_start(offs_t[:], offs)
+        for q in range(4):
+            nc.sync.dma_start(
+                out=x_scale_landing[32 * q : 32 * q + 4 * PASSES, :],
+                in_=x_scales[:, 4 * q : 4 * q + 4, :].bitcast(I32),
+            )
+        nc.sync.dma_start(out=w1_first[:], in_=w1_rows[0])
+        for u in range(2):
+            nc.sync.dma_start(out=w1_second[u][:], in_=w1_rows[1][:, :, u * HALF : (u + 1) * HALF])
+        for g in range(PASSES):
+            nc.sync.dma_start(out=x_window[g][:], in_=x_words[g].rearrange("p n t -> p (n t)").bitcast(I32))
+        nc.sync.dma_start(pos1_t[:], pos1)
+        nc.sync.dma_start(pos2_t[:], pos2)
+        for w, scales in enumerate((w2_scales, w3_scales)):
+            for q in range(4):
+                nc.sync.dma_start(
+                    out=head_scale_rows[w][32 * q : 32 * q + 4, :].bitcast(I32),
+                    in_=scales[0, 4 * q : 4 * q + 4, :].bitcast(I32),
+                )
+
+        head_dealt = [keep.tile([P, 2 * N], U8, name=f"head_dealt{w}", align_bytes=64) for w in range(2)]
+        head_scales = [None, None]
+
+        def deal_words(w):
+            nc.vector.tensor_copy(
+                out=head_dealt[w][:].rearrange("p (t m b) -> p t m b", t=PACK, b=2),
+                in_=head_words[w][:].rearrange("p (m t b) -> p t m b", t=PACK, b=2),
+            )
+
+        def deal_scales(w, tag):
+            head_scales[w] = keep.tile([P, N], U8, name=f"head_scales{w}", tag=tag, align_bytes=64)
+            nc.vector.tensor_copy(
+                out=head_scales[w][:].rearrange("p (t m) -> p t m", t=PACK),
+                in_=head_scale_rows[w][:].rearrange("p (m t) -> p t m", t=PACK),
+            )
+
+        deal_words(0)
+        deal_words(1)
+        for q in range(4):
+            live = slice(32 * q, 32 * q + 4 * PASSES)
+            nc.vector.tensor_copy(out=x_scale_rows[live, :].bitcast(I32), in_=x_scale_landing[live, :])
+        x_scales_picked = keep.tile([P, S], U8, align_bytes=64)
+        nc.vector.tensor_copy(x_scales_picked[:], x_scale_rows[:].indirect(offs_t[:]))
+
+        w1_grouped = [keep.tile([P, PACK, P, PACK], BF16, name=f"w1_grouped{g}", align_bytes=64) for g in range(PASSES)]
+        w1_codes = [keep.tile([P, H], U32, name=f"w1_codes{g}", align_bytes=64) for g in range(PASSES)]
+        w1_scales = [keep.tile([P, H], U8, name=f"w1_scales{g}", align_bytes=64) for g in range(PASSES)]
+
+        def round_w1(g, u, copy):
+            copy(
+                out=w1_grouped[g][:, :, u * (P // 2) : (u + 1) * (P // 2), :].rearrange("p t m j -> p m j t"),
+                in_=w1_raw[g][u].rearrange("p j (m t) -> p m j t", t=PACK),
+            )
+
+        def quantize_w1(g):
+            nc.vector.quantize_mx(
+                out=w1_codes[g][:].bitcast(FP8X4),
+                scales=w1_scales[g][:],
+                in_=w1_grouped[g][:].rearrange("p t m j -> p (t m j)"),
+            )
+
+        round_w1(0, 0, nc.scalar.copy)
+        round_w1(0, 1, nc.vector.tensor_copy)
+        round_w1(1, 0, nc.scalar.copy)
+        quantize_w1(0)
+        round_w1(1, 1, nc.vector.tensor_copy)
+        quantize_w1(1)
+
+        hidden = [hidden_psum.tile([P, PACK, BLOCK], F32, name=f"hidden{b}") for b in range(BLOCKS)]
+        x_picked = [
+            [keep.tile([P, BLOCK], U32, name=f"x_picked{g}{b}", align_bytes=64) for b in range(BLOCKS)]
+            for g in range(PASSES)
+        ]
+
+        def pick_words(g, b):
+            nc.vector.tensor_copy(
+                x_picked[g][b][:],
+                x_window[g][:].bitcast(U32).indirect(offs_t[:, b * BLOCK // 16 : (b + 1) * BLOCK // 16]),
+            )
+
+        h_codes = keep.tile([P, S], U32, align_bytes=64)
+        h_scales = keep.tile([P, S], U8, align_bytes=64)
+
+        def first_layer_pass(b, t, g):
+            cols = slice(b * BLOCK, (b + 1) * BLOCK)
+            nc.tensor.matmul_mx(
+                out=hidden[b][:, t, :],
+                lhsT=w1_codes[g][:, t * P : (t + 1) * P].bitcast(FP8X4),
+                lhsT_scale=w1_scales[g][:, t * P : (t + 1) * P],
+                rhs=x_picked[g][b][:].bitcast(FP8X4),
+                rhs_scale=x_scales_picked[4 * g : P, cols],
+                start=(g == 0),
+                stop=(g == PASSES - 1),
+            )
+
+        for b in range(BLOCKS):
+            pick_words(0, b)
+            first_layer_pass(b, 0, 0)
+        for b in range(BLOCKS):
+            pick_words(1, b)
+        for b in range(BLOCKS):
+            cols = slice(b * BLOCK, (b + 1) * BLOCK)
+            first_layer_pass(b, 0, 1)
+            for t in range(1, PACK):
+                for g in range(PASSES):
+                    first_layer_pass(b, t, g)
+            h_grouped = keep.tile([P, BLOCK, PACK], BF16, name=f"h_grouped{b}", tag=f"h_grouped{b}", align_bytes=64)
+            nc.scalar.activation(out=h_grouped[:], in_=hidden[b][:].rearrange("p t j -> p j t"), func=ACT.Relu)
+            nc.vector.quantize_mx(
+                out=h_codes[:, cols].bitcast(FP8X4),
+                scales=h_scales[:, cols],
+                in_=h_grouped[:].rearrange("p j t -> p (j t)"),
+            )
+
+        def head_columns(rows, w, t, cols, copy):
+            acc = head_psum.tile([P, S], F32, name="acc")
+            nc.tensor.matmul_mx(
+                out=acc[:, cols],
+                lhsT=head_dealt[w][:, t * 2 * P : (t + 1) * 2 * P].bitcast(FP4X4),
+                lhsT_scale=head_scales[w][:, t * P : (t + 1) * P],
+                rhs=h_codes[:, cols].bitcast(FP8X4),
+                rhs_scale=h_scales[:, cols],
+                start=True,
+                stop=True,
+            )
+            copy(out=rows[:, cols], in_=acc[:, cols])
+
+        score = [keep.tile([P, S], F32, name=f"score{t}") for t in range(PACK)]
+        feature = [keep.tile([P, S], F32, name=f"feature{t}") for t in range(PACK)]
+
+        def make_score(t):
+            head_columns(score[t], 0, t, slice(0, S), nc.scalar.copy)
+
+        def make_feature(t):
+            head_columns(feature[t], 1, t, slice(0, S), nc.scalar.copy)
+
+        def scratch(name, t):
+            return keep.tile([P, V], F32, name=f"{name}{t}")
+
+        pooled = keep.tile([P, PACK, V], F32)
+        out_rows = out_0.rearrange("(p t) v -> p t v", t=PACK)
+        weight0 = [scratch("weight0_", 0)[:]] + [pooled[:, t, :] for t in range(PACK - 1)]
+        weight1 = [scratch("weight1_", t) for t in range(PACK)]
+        first_score = [scratch("first_score", t) for t in range(PACK)]
+        gap = [scratch("gap", t) for t in range(PACK)]
+        term0 = [scratch("term0_", t) for t in range(PACK)]
+        term1 = [scratch("term1_", t) for t in range(PACK)]
+        whole = slice(0, V)
+        halves = (slice(0, V // 2), slice(V // 2, V))
+
+        def entries(positions, part):
+            return positions[:, part.start // 16 : part.stop // 16]
+
+        def score_gap(t):
+            for part in halves:
+                nc.vector.tensor_copy(first_score[t][:, part], score[t][:].indirect(entries(pos1_t, part)))
+            for part in halves:
+                nc.vector.tensor_tensor(
+                    gap[t][:, part], score[t][:].indirect(entries(pos2_t, part)), first_score[t][:, part], ALU.subtract
+                )
+
+        def make_weights(t):
+            nc.scalar.activation(out=weight0[t], in_=gap[t][:], func=ACT.Sigmoid, scale=-1.0)
+            nc.scalar.activation(out=weight1[t][:], in_=gap[t][:], func=ACT.Sigmoid)
+
+        def weigh0(t):
+            nc.vector.tensor_tensor(term0[t][:], feature[t][:].indirect(pos1_t[:]), weight0[t], ALU.mult)
+
+        def weigh1(t, part):
+            nc.vector.tensor_tensor(
+                term1[t][:, part],
+                feature[t][:].indirect(pos2_t[:, part.start // 16 : part.stop // 16]),
+                weight1[t][:, part],
+                ALU.mult,
+            )
+
+        def pool(t, part):
+            nc.vector.tensor_tensor(pooled[:, t, part], term0[t][:, part], term1[t][:, part], ALU.add)
+
+        def store(t):
+            nc.sync.dma_start(out=out_rows[:, t, :], in_=pooled[:, t, :])
+
+        deal_scales(0, "h_grouped0")
+        head_columns(score[0], 0, 0, slice(0, S // 2), nc.vector.tensor_copy)
+        deal_scales(1, "h_grouped1")
+        head_columns(score[0], 0, 0, slice(S // 2, S), nc.scalar.copy)
+        for t in range(1, PACK):
+            make_score(t)
+        for t in range(PACK):
+            score_gap(t)
+        for t in range(PACK):
+            make_feature(t)
+            make_weights(t)
+            weigh0(t)
+            if t >= 1:
+                pool(t - 1, whole)
+                store(t - 1)
+            if t + 1 < PACK:
+                weigh1(t, whole)
+
+        out_grouped = keep.tile([P, V, PACK], BF16, align_bytes=64)
+        out_codes = keep.tile([P, V], U32, align_bytes=64)
+        out_scales = keep.tile([P, V], U8, align_bytes=64)
+
+        def round_pair(first, part, copy):
+            copy(
+                out=out_grouped[:, part, first : first + 2],
+                in_=pooled[:, first : first + 2, part].rearrange("p t v -> p v t"),
+            )
+
+        round_pair(0, whole, nc.scalar.copy)
+        for part in halves:
+            weigh1(PACK - 1, part)
+        for part in halves:
+            pool(PACK - 1, part)
+        store(PACK - 1)
+        for part in halves:
+            round_pair(2, part, nc.vector.tensor_copy)
+        for part in halves:
+            nc.vector.quantize_mx(
+                out=out_codes[:, part].bitcast(FP8X4),
+                scales=out_scales[:, part],
+                in_=out_grouped[:, part, :].rearrange("p v t -> p (v t)"),
+            )
+        nc.sync.dma_start(out=out_1[0].rearrange("p c r -> p (c r)").bitcast(I32), in_=out_codes[:].bitcast(I32))
+        for q in range(4):
+            queue = nc.scalar if q % 2 else nc.sync
+            queue.dma_start(
+                out=out_2[0, 4 * q : 4 * q + 4, :].bitcast(I32),
+                in_=out_scales[32 * q : 32 * q + 4, :].bitcast(I32),
+            )

@@ -22,6 +22,7 @@ PASSES = K // (P * PACK)
 BLOCK = 128
 BLOCKS = S // BLOCK
 HALF = H // 2
+LAST_SCALAR_SHARE = 22
 
 
 def tile_picked_zrandla_relu_po_kernel(
@@ -44,9 +45,7 @@ def tile_picked_zrandla_relu_po_kernel(
         for w in range(2):
             nc.gpsimd.memset(head_scale_rows[w][:].bitcast(I32), 0)
 
-        w1_first = keep.tile([P, PACK, H], F32)
-        w1_second = [keep.tile([P, PACK, HALF], F32, name=f"w1_second{u}") for u in range(2)]
-        w1_raw = [[w1_first[:, :, u * HALF : (u + 1) * HALF] for u in range(2)], [w1_second[u][:] for u in range(2)]]
+        w1_raw = [[keep.tile([P, PACK, HALF], F32, name=f"w1_raw{g}{u}") for u in range(2)] for g in range(PASSES)]
         w1_rows = w1.rearrange("(g p j) c -> g p j c", p=P, j=PACK)
         x_window = [keep.tile([P, T], I32, name=f"x_window{g}", align_bytes=64) for g in range(PASSES)]
         x_scale_landing = keep.tile([P, T // 4], I32)
@@ -54,19 +53,29 @@ def tile_picked_zrandla_relu_po_kernel(
         pos1_t = lists.tile([P, V // 16], U16)
         pos2_t = lists.tile([P, V // 16], U16)
 
-        for w, words in enumerate((w2_words, w3_words)):
+        def load_head_words(w, words):
             nc.sync.dma_start(out=head_words[w][:].bitcast(I32), in_=words[0].bitcast(I32))
+
+        def load_w1(g, u):
+            nc.sync.dma_start(out=w1_raw[g][u][:], in_=w1_rows[g][:, :, u * HALF : (u + 1) * HALF])
+
+        def load_x(g):
+            nc.sync.dma_start(out=x_window[g][:], in_=x_words[g].rearrange("p n t -> p (n t)").bitcast(I32))
+
+        load_head_words(0, w2_words)
+        load_w1(0, 0)
         nc.sync.dma_start(offs_t[:], offs)
         for q in range(4):
             nc.sync.dma_start(
                 out=x_scale_landing[32 * q : 32 * q + 4 * PASSES, :],
                 in_=x_scales[:, 4 * q : 4 * q + 4, :].bitcast(I32),
             )
-        nc.sync.dma_start(out=w1_first[:], in_=w1_rows[0])
-        for u in range(2):
-            nc.sync.dma_start(out=w1_second[u][:], in_=w1_rows[1][:, :, u * HALF : (u + 1) * HALF])
-        for g in range(PASSES):
-            nc.sync.dma_start(out=x_window[g][:], in_=x_words[g].rearrange("p n t -> p (n t)").bitcast(I32))
+        load_w1(0, 1)
+        load_x(0)
+        load_head_words(1, w3_words)
+        load_w1(1, 0)
+        load_w1(1, 1)
+        load_x(1)
         nc.sync.dma_start(pos1_t[:], pos1)
         nc.sync.dma_start(pos2_t[:], pos2)
         for w, scales in enumerate((w2_scales, w3_scales)):
@@ -93,7 +102,6 @@ def tile_picked_zrandla_relu_po_kernel(
             )
 
         deal_words(0)
-        deal_words(1)
         for q in range(4):
             live = slice(32 * q, 32 * q + 4 * PASSES)
             nc.vector.tensor_copy(out=x_scale_rows[live, :].bitcast(I32), in_=x_scale_landing[live, :])
@@ -104,10 +112,10 @@ def tile_picked_zrandla_relu_po_kernel(
         w1_codes = [keep.tile([P, H], U32, name=f"w1_codes{g}", align_bytes=64) for g in range(PASSES)]
         w1_scales = [keep.tile([P, H], U8, name=f"w1_scales{g}", align_bytes=64) for g in range(PASSES)]
 
-        def round_w1(g, u, copy):
+        def round_w1(g, u, first, last, copy):
             copy(
-                out=w1_grouped[g][:, :, u * (P // 2) : (u + 1) * (P // 2), :].rearrange("p t m j -> p m j t"),
-                in_=w1_raw[g][u].rearrange("p j (m t) -> p m j t", t=PACK),
+                out=w1_grouped[g][:, :, u * P // 2 + first : u * P // 2 + last, :].rearrange("p t m j -> p m j t"),
+                in_=w1_raw[g][u][:, :, PACK * first : PACK * last].rearrange("p j (m t) -> p m j t", t=PACK),
             )
 
         def quantize_w1(g):
@@ -117,23 +125,18 @@ def tile_picked_zrandla_relu_po_kernel(
                 in_=w1_grouped[g][:].rearrange("p t m j -> p (t m j)"),
             )
 
-        round_w1(0, 0, nc.scalar.copy)
-        round_w1(0, 1, nc.vector.tensor_copy)
-        round_w1(1, 0, nc.scalar.copy)
-        quantize_w1(0)
-        round_w1(1, 1, nc.vector.tensor_copy)
-        quantize_w1(1)
+        round_w1(0, 0, 0, P // 2, nc.scalar.copy)
+        round_w1(0, 1, 0, P // 2, nc.scalar.copy)
+        round_w1(1, 0, 0, P // 2, nc.scalar.copy)
+        round_w1(1, 1, 0, LAST_SCALAR_SHARE, nc.scalar.copy)
 
         hidden = [hidden_psum.tile([P, PACK, BLOCK], F32, name=f"hidden{b}") for b in range(BLOCKS)]
-        x_picked = [
-            [keep.tile([P, BLOCK], U32, name=f"x_picked{g}{b}", align_bytes=64) for b in range(BLOCKS)]
-            for g in range(PASSES)
-        ]
+        x_picked = [keep.tile([P, S], U32, name=f"x_picked{g}", align_bytes=64) for g in range(PASSES)]
 
-        def pick_words(g, b):
+        def pick_words(g, first, last):
             nc.vector.tensor_copy(
-                x_picked[g][b][:],
-                x_window[g][:].bitcast(U32).indirect(offs_t[:, b * BLOCK // 16 : (b + 1) * BLOCK // 16]),
+                x_picked[g][:, first:last],
+                x_window[g][:].bitcast(U32).indirect(offs_t[:, first // 16 : last // 16]),
             )
 
         h_codes = keep.tile([P, S], U32, align_bytes=64)
@@ -145,17 +148,32 @@ def tile_picked_zrandla_relu_po_kernel(
                 out=hidden[b][:, t, :],
                 lhsT=w1_codes[g][:, t * P : (t + 1) * P].bitcast(FP8X4),
                 lhsT_scale=w1_scales[g][:, t * P : (t + 1) * P],
-                rhs=x_picked[g][b][:].bitcast(FP8X4),
+                rhs=x_picked[g][:, cols].bitcast(FP8X4),
                 rhs_scale=x_scales_picked[4 * g : P, cols],
                 start=(g == 0),
                 stop=(g == PASSES - 1),
             )
 
+        pick_words(0, 0, S)
+        quantize_w1(0)
         for b in range(BLOCKS):
-            pick_words(0, b)
             first_layer_pass(b, 0, 0)
+        warm_psum = head_psum.tile([P, S], F32, name="acc")
+        for width in (S, S // 2):
+            nc.tensor.matmul_mx(
+                out=warm_psum[:, :width],
+                lhsT=w1_codes[0][:, :P].bitcast(FP8X4),
+                lhsT_scale=w1_scales[0][:, :P],
+                rhs=w1_codes[0][:, :width].bitcast(FP8X4),
+                rhs_scale=w1_scales[0][:, :width],
+                start=True,
+                stop=True,
+            )
+        deal_words(1)
+        round_w1(1, 1, LAST_SCALAR_SHARE, P // 2, nc.vector.tensor_copy)
+        quantize_w1(1)
         for b in range(BLOCKS):
-            pick_words(1, b)
+            pick_words(1, b * BLOCK, (b + 1) * BLOCK)
         for b in range(BLOCKS):
             cols = slice(b * BLOCK, (b + 1) * BLOCK)
             first_layer_pass(b, 0, 1)
@@ -241,7 +259,8 @@ def tile_picked_zrandla_relu_po_kernel(
         deal_scales(0, "h_grouped0")
         head_columns(score[0], 0, 0, slice(0, S // 2), nc.vector.tensor_copy)
         deal_scales(1, "h_grouped1")
-        head_columns(score[0], 0, 0, slice(S // 2, S), nc.scalar.copy)
+        head_columns(score[0], 0, 0, slice(2 * BLOCK, 3 * BLOCK), nc.vector.tensor_copy)
+        head_columns(score[0], 0, 0, slice(3 * BLOCK, S), nc.scalar.copy)
         for t in range(1, PACK):
             make_score(t)
         for t in range(PACK):

@@ -217,23 +217,17 @@ def tile_picked_zrandla_relu_po_kernel(
         out_rows = out_0.rearrange("(p t) v -> p t v", t=PACK)
         weight0 = [scratch("weight0_", 0)[:]] + [pooled[:, t, :] for t in range(PACK - 1)]
         weight1 = [scratch("weight1_", t) for t in range(PACK)]
-        first_score = [scratch("first_score", t) for t in range(PACK)]
+        score_pair = [[scratch(f"score_at{d}_", t) for d in range(2)] for t in range(PACK)]
         gap = [scratch("gap", t) for t in range(PACK)]
         term0 = [scratch("term0_", t) for t in range(PACK)]
         term1 = [scratch("term1_", t) for t in range(PACK)]
         whole = slice(0, V)
         halves = (slice(0, V // 2), slice(V // 2, V))
 
-        def entries(positions, part):
-            return positions[:, part.start // 16 : part.stop // 16]
-
         def score_gap(t):
-            for part in halves:
-                nc.vector.tensor_copy(first_score[t][:, part], score[t][:].indirect(entries(pos1_t, part)))
-            for part in halves:
-                nc.vector.tensor_tensor(
-                    gap[t][:, part], score[t][:].indirect(entries(pos2_t, part)), first_score[t][:, part], ALU.subtract
-                )
+            for d, positions in enumerate((pos1_t, pos2_t)):
+                nc.vector.tensor_copy(score_pair[t][d][:], score[t][:].indirect(positions[:]))
+            nc.gpsimd.tensor_tensor(gap[t][:], score_pair[t][1][:], score_pair[t][0][:], ALU.subtract)
 
         def make_weights(t):
             nc.scalar.activation(out=weight0[t], in_=gap[t][:], func=ACT.Sigmoid, scale=-1.0)

@@ -21,8 +21,7 @@ PACK = 4
 PASSES = K // (P * PACK)
 BLOCK = 128
 BLOCKS = S // BLOCK
-HALF = H // 2
-LAST_SCALAR_SHARE = 22
+LAST_SCALAR_SHARE = 46
 
 
 def tile_picked_zrandla_relu_po_kernel(
@@ -45,7 +44,7 @@ def tile_picked_zrandla_relu_po_kernel(
         for w in range(2):
             nc.gpsimd.memset(head_scale_rows[w][:].bitcast(I32), 0)
 
-        w1_raw = [[keep.tile([P, PACK, HALF], F32, name=f"w1_raw{g}{u}") for u in range(2)] for g in range(PASSES)]
+        w1_raw = [keep.tile([P, PACK, H], F32, name=f"w1_raw{g}") for g in range(PASSES)]
         w1_rows = w1.rearrange("(g p j) c -> g p j c", p=P, j=PACK)
         x_window = [keep.tile([P, T], I32, name=f"x_window{g}", align_bytes=64) for g in range(PASSES)]
         x_scale_landing = keep.tile([P, T // 4], I32)
@@ -53,29 +52,17 @@ def tile_picked_zrandla_relu_po_kernel(
         pos1_t = lists.tile([P, V // 16], U16)
         pos2_t = lists.tile([P, V // 16], U16)
 
-        def load_head_words(w, words):
+        for w, words in enumerate((w2_words, w3_words)):
             nc.sync.dma_start(out=head_words[w][:].bitcast(I32), in_=words[0].bitcast(I32))
-
-        def load_w1(g, u):
-            nc.sync.dma_start(out=w1_raw[g][u][:], in_=w1_rows[g][:, :, u * HALF : (u + 1) * HALF])
-
-        def load_x(g):
-            nc.sync.dma_start(out=x_window[g][:], in_=x_words[g].rearrange("p n t -> p (n t)").bitcast(I32))
-
-        load_head_words(0, w2_words)
-        load_w1(0, 0)
         nc.sync.dma_start(offs_t[:], offs)
         for q in range(4):
             nc.sync.dma_start(
                 out=x_scale_landing[32 * q : 32 * q + 4 * PASSES, :],
                 in_=x_scales[:, 4 * q : 4 * q + 4, :].bitcast(I32),
             )
-        load_w1(0, 1)
-        load_x(0)
-        load_head_words(1, w3_words)
-        load_w1(1, 0)
-        load_w1(1, 1)
-        load_x(1)
+        for g in range(PASSES):
+            nc.sync.dma_start(out=w1_raw[g][:], in_=w1_rows[g])
+            nc.sync.dma_start(out=x_window[g][:], in_=x_words[g].rearrange("p n t -> p (n t)").bitcast(I32))
         nc.sync.dma_start(pos1_t[:], pos1)
         nc.sync.dma_start(pos2_t[:], pos2)
         for w, scales in enumerate((w2_scales, w3_scales)):
@@ -102,6 +89,7 @@ def tile_picked_zrandla_relu_po_kernel(
             )
 
         deal_words(0)
+        deal_words(1)
         for q in range(4):
             live = slice(32 * q, 32 * q + 4 * PASSES)
             nc.vector.tensor_copy(out=x_scale_rows[live, :].bitcast(I32), in_=x_scale_landing[live, :])
@@ -112,10 +100,10 @@ def tile_picked_zrandla_relu_po_kernel(
         w1_codes = [keep.tile([P, H], U32, name=f"w1_codes{g}", align_bytes=64) for g in range(PASSES)]
         w1_scales = [keep.tile([P, H], U8, name=f"w1_scales{g}", align_bytes=64) for g in range(PASSES)]
 
-        def round_w1(g, u, first, last, copy):
+        def round_w1(g, first, last, copy):
             copy(
-                out=w1_grouped[g][:, :, u * P // 2 + first : u * P // 2 + last, :].rearrange("p t m j -> p m j t"),
-                in_=w1_raw[g][u][:, :, PACK * first : PACK * last].rearrange("p j (m t) -> p m j t", t=PACK),
+                out=w1_grouped[g][:, :, first:last, :].rearrange("p t m j -> p m j t"),
+                in_=w1_raw[g][:, :, PACK * first : PACK * last].rearrange("p j (m t) -> p m j t", t=PACK),
             )
 
         def quantize_w1(g):
@@ -125,10 +113,8 @@ def tile_picked_zrandla_relu_po_kernel(
                 in_=w1_grouped[g][:].rearrange("p t m j -> p (t m j)"),
             )
 
-        round_w1(0, 0, 0, P // 2, nc.scalar.copy)
-        round_w1(0, 1, 0, P // 2, nc.scalar.copy)
-        round_w1(1, 0, 0, P // 2, nc.scalar.copy)
-        round_w1(1, 1, 0, LAST_SCALAR_SHARE, nc.scalar.copy)
+        round_w1(0, 0, P, nc.scalar.copy)
+        round_w1(1, 0, LAST_SCALAR_SHARE, nc.scalar.copy)
 
         hidden = [hidden_psum.tile([P, PACK, BLOCK], F32, name=f"hidden{b}") for b in range(BLOCKS)]
         x_picked = [keep.tile([P, S], U32, name=f"x_picked{g}", align_bytes=64) for g in range(PASSES)]
@@ -169,8 +155,7 @@ def tile_picked_zrandla_relu_po_kernel(
                 start=True,
                 stop=True,
             )
-        deal_words(1)
-        round_w1(1, 1, LAST_SCALAR_SHARE, P // 2, nc.vector.tensor_copy)
+        round_w1(1, LAST_SCALAR_SHARE, P, nc.vector.tensor_copy)
         quantize_w1(1)
         for b in range(BLOCKS):
             pick_words(1, b * BLOCK, (b + 1) * BLOCK)
@@ -217,17 +202,23 @@ def tile_picked_zrandla_relu_po_kernel(
         out_rows = out_0.rearrange("(p t) v -> p t v", t=PACK)
         weight0 = [scratch("weight0_", 0)[:]] + [pooled[:, t, :] for t in range(PACK - 1)]
         weight1 = [scratch("weight1_", t) for t in range(PACK)]
-        score_pair = [[scratch(f"score_at{d}_", t) for d in range(2)] for t in range(PACK)]
+        first_score = [scratch("first_score", t) for t in range(PACK)]
         gap = [scratch("gap", t) for t in range(PACK)]
         term0 = [scratch("term0_", t) for t in range(PACK)]
         term1 = [scratch("term1_", t) for t in range(PACK)]
         whole = slice(0, V)
         halves = (slice(0, V // 2), slice(V // 2, V))
 
+        def entries(positions, part):
+            return positions[:, part.start // 16 : part.stop // 16]
+
         def score_gap(t):
-            for d, positions in enumerate((pos1_t, pos2_t)):
-                nc.vector.tensor_copy(score_pair[t][d][:], score[t][:].indirect(positions[:]))
-            nc.gpsimd.tensor_tensor(gap[t][:], score_pair[t][1][:], score_pair[t][0][:], ALU.subtract)
+            for part in halves:
+                nc.vector.tensor_copy(first_score[t][:, part], score[t][:].indirect(entries(pos1_t, part)))
+            for part in halves:
+                nc.vector.tensor_tensor(
+                    gap[t][:, part], score[t][:].indirect(entries(pos2_t, part)), first_score[t][:, part], ALU.subtract
+                )
 
         def make_weights(t):
             nc.scalar.activation(out=weight0[t], in_=gap[t][:], func=ACT.Sigmoid, scale=-1.0)

@@ -1,6 +1,7 @@
 from contextlib import ExitStack
 
 import concourse.mybir as mybir
+from concourse.masks import make_identity
 
 K, T, S, V, H, N = 1024, 1024, 512, 256, 512, 512
 FLOPS = 2 * S * (K * H + 2 * H * N)
@@ -21,7 +22,9 @@ PACK = 4
 PASSES = K // (P * PACK)
 BLOCK = 128
 BLOCKS = S // BLOCK
-LAST_SCALAR_SHARE = 46
+VECTOR_RELU_BLOCK = 3
+QUADRANT_ORDER = (0, 2, 1, 3)
+SUMMED_ON_TENSOR = 2
 
 
 def tile_picked_zrandla_relu_po_kernel(
@@ -36,15 +39,15 @@ def tile_picked_zrandla_relu_po_kernel(
 
         head_words = [keep.tile([P, 2 * N], U8, name=f"head_words{w}", align_bytes=64) for w in range(2)]
         x_scale_rows = keep.tile([P, T], U8, align_bytes=64)
-        nc.gpsimd.memset(x_scale_rows[:].bitcast(I32), 0)
         warm = keep.tile([P, 2], F32)
-        nc.gpsimd.memset(warm[:, 0:1], 0.0)
+        nc.vector.memset(warm[:, 0:1], 0.0)
         nc.scalar.activation(out=warm[:, 1:2], in_=warm[:, 0:1], func=ACT.Sigmoid)
         head_scale_rows = [keep.tile([P, N], U8, name=f"head_scale_rows{w}", align_bytes=64) for w in range(2)]
-        for w in range(2):
-            nc.gpsimd.memset(head_scale_rows[w][:].bitcast(I32), 0)
+        nc.vector.memset(head_scale_rows[0][:].bitcast(I32), 0)
+        nc.gpsimd.memset(x_scale_rows[:].bitcast(I32), 0)
+        nc.gpsimd.memset(head_scale_rows[1][:].bitcast(I32), 0)
 
-        w1_raw = [keep.tile([P, PACK, H], F32, name=f"w1_raw{g}") for g in range(PASSES)]
+        w1_raw = [keep.tile([P, PACK, H], F32, name=f"w1_raw{g}", align_bytes=64) for g in range(PASSES)]
         w1_rows = w1.rearrange("(g p j) c -> g p j c", p=P, j=PACK)
         x_window = [keep.tile([P, T], I32, name=f"x_window{g}", align_bytes=64) for g in range(PASSES)]
         x_scale_landing = keep.tile([P, T // 4], I32)
@@ -52,30 +55,37 @@ def tile_picked_zrandla_relu_po_kernel(
         pos1_t = lists.tile([P, V // 16], U16)
         pos2_t = lists.tile([P, V // 16], U16)
 
-        for w, words in enumerate((w2_words, w3_words)):
-            nc.sync.dma_start(out=head_words[w][:].bitcast(I32), in_=words[0].bitcast(I32))
+        nc.sync.dma_start(out=head_words[0][:].bitcast(I32), in_=w2_words[0].bitcast(I32))
         nc.sync.dma_start(offs_t[:], offs)
-        for q in range(4):
+        for q in QUADRANT_ORDER:
             nc.sync.dma_start(
                 out=x_scale_landing[32 * q : 32 * q + 4 * PASSES, :],
                 in_=x_scales[:, 4 * q : 4 * q + 4, :].bitcast(I32),
             )
-        for g in range(PASSES):
-            nc.sync.dma_start(out=w1_raw[g][:], in_=w1_rows[g])
-            nc.sync.dma_start(out=x_window[g][:], in_=x_words[g].rearrange("p n t -> p (n t)").bitcast(I32))
-        nc.sync.dma_start(pos1_t[:], pos1)
-        nc.sync.dma_start(pos2_t[:], pos2)
-        for w, scales in enumerate((w2_scales, w3_scales)):
-            for q in range(4):
-                nc.sync.dma_start(
+        def load_head_scales(w, scales, queue, quadrants):
+            for q in quadrants:
+                queue.dma_start(
                     out=head_scale_rows[w][32 * q : 32 * q + 4, :].bitcast(I32),
                     in_=scales[0, 4 * q : 4 * q + 4, :].bitcast(I32),
                 )
 
-        head_dealt = [keep.tile([P, 2 * N], U8, name=f"head_dealt{w}", align_bytes=64) for w in range(2)]
+        for g in range(PASSES):
+            nc.sync.dma_start(out=w1_raw[g][:], in_=w1_rows[g])
+            nc.sync.dma_start(out=x_window[g][:], in_=x_words[g].rearrange("p n t -> p (n t)").bitcast(I32))
+            if g == 0:
+                load_head_scales(0, w2_scales, nc.sync, QUADRANT_ORDER)
+        nc.sync.dma_start(out=head_words[1][:].bitcast(I32), in_=w3_words[0].bitcast(I32))
+        load_head_scales(1, w3_scales, nc.sync, QUADRANT_ORDER)
+        nc.sync.dma_start(pos1_t[:], pos1)
+        nc.sync.dma_start(pos2_t[:], pos2)
+        identity = keep.tile([P, P], F32)
+        make_identity(nc, identity[:])
+
+        head_dealt = [None, None]
         head_scales = [None, None]
 
-        def deal_words(w):
+        def deal_words(w, tag):
+            head_dealt[w] = keep.tile([P, 2 * N], U8, name=f"head_dealt{w}", tag=tag, align_bytes=64)
             nc.vector.tensor_copy(
                 out=head_dealt[w][:].rearrange("p (t m b) -> p t m b", t=PACK, b=2),
                 in_=head_words[w][:].rearrange("p (m t b) -> p t m b", t=PACK, b=2),
@@ -88,8 +98,7 @@ def tile_picked_zrandla_relu_po_kernel(
                 in_=head_scale_rows[w][:].rearrange("p (m t) -> p t m", t=PACK),
             )
 
-        deal_words(0)
-        deal_words(1)
+        deal_words(0, "head_dealt0")
         for q in range(4):
             live = slice(32 * q, 32 * q + 4 * PASSES)
             nc.vector.tensor_copy(out=x_scale_rows[live, :].bitcast(I32), in_=x_scale_landing[live, :])
@@ -100,21 +109,26 @@ def tile_picked_zrandla_relu_po_kernel(
         w1_codes = [keep.tile([P, H], U32, name=f"w1_codes{g}", align_bytes=64) for g in range(PASSES)]
         w1_scales = [keep.tile([P, H], U8, name=f"w1_scales{g}", align_bytes=64) for g in range(PASSES)]
 
-        def round_w1(g, first, last, copy):
+        def round_w1(g, tiles, first, last, copy):
             copy(
-                out=w1_grouped[g][:, :, first:last, :].rearrange("p t m j -> p m j t"),
-                in_=w1_raw[g][:, :, PACK * first : PACK * last].rearrange("p j (m t) -> p m j t", t=PACK),
+                out=w1_grouped[g][:, tiles, first:last, :].rearrange("p t m j -> p m j t"),
+                in_=w1_raw[g][:, :, PACK * first : PACK * last].rearrange("p j (m t) -> p m j t", t=PACK)[
+                    :, :, :, tiles
+                ],
             )
 
-        def quantize_w1(g):
+        def quantize_w1(g, tiles):
+            cols = slice(tiles.start * P, tiles.stop * P)
             nc.vector.quantize_mx(
-                out=w1_codes[g][:].bitcast(FP8X4),
-                scales=w1_scales[g][:],
-                in_=w1_grouped[g][:].rearrange("p t m j -> p (t m j)"),
+                out=w1_codes[g][:, cols].bitcast(FP8X4),
+                scales=w1_scales[g][:, cols],
+                in_=w1_grouped[g][:, tiles].rearrange("p t m j -> p (t m j)"),
             )
 
-        round_w1(0, 0, P, nc.scalar.copy)
-        round_w1(1, 0, LAST_SCALAR_SHARE, nc.scalar.copy)
+        low_tiles, high_tiles = slice(0, 2), slice(2, PACK)
+        round_w1(0, low_tiles, 0, P, nc.scalar.copy)
+        round_w1(0, high_tiles, 0, P, nc.scalar.copy)
+        round_w1(1, high_tiles, 0, P, nc.scalar.copy)
 
         hidden = [hidden_psum.tile([P, PACK, BLOCK], F32, name=f"hidden{b}") for b in range(BLOCKS)]
         x_picked = [keep.tile([P, S], U32, name=f"x_picked{g}", align_bytes=64) for g in range(PASSES)]
@@ -136,74 +150,72 @@ def tile_picked_zrandla_relu_po_kernel(
                 lhsT_scale=w1_scales[g][:, t * P : (t + 1) * P],
                 rhs=x_picked[g][:, cols].bitcast(FP8X4),
                 rhs_scale=x_scales_picked[4 * g : P, cols],
-                start=(g == 0),
-                stop=(g == PASSES - 1),
+                start=(g == 0 and t == 0),
+                stop=(g == PASSES - 1 and t == PACK - 1),
             )
 
         pick_words(0, 0, S)
-        quantize_w1(0)
-        for b in range(BLOCKS):
-            first_layer_pass(b, 0, 0)
-        warm_psum = head_psum.tile([P, S], F32, name="acc")
-        for width in (S, S // 2):
-            nc.tensor.matmul_mx(
-                out=warm_psum[:, :width],
-                lhsT=w1_codes[0][:, :P].bitcast(FP8X4),
-                lhsT_scale=w1_scales[0][:, :P],
-                rhs=w1_codes[0][:, :width].bitcast(FP8X4),
-                rhs_scale=w1_scales[0][:, :width],
-                start=True,
-                stop=True,
-            )
-        round_w1(1, LAST_SCALAR_SHARE, P, nc.vector.tensor_copy)
-        quantize_w1(1)
-        for b in range(BLOCKS):
+        quantize_w1(0, low_tiles)
+        quantize_w1(0, high_tiles)
+        deal_scales(0, "head_scales0")
+        for t in range(PACK):
+            for b in range(BLOCKS):
+                first_layer_pass(b, t, 0)
+        round_w1(1, low_tiles, 0, P, nc.vector.tensor_copy)
+        quantize_w1(1, low_tiles)
+        pick_words(1, 0, BLOCK)
+        quantize_w1(1, high_tiles)
+        for b in range(1, BLOCKS):
             pick_words(1, b * BLOCK, (b + 1) * BLOCK)
         for b in range(BLOCKS):
             cols = slice(b * BLOCK, (b + 1) * BLOCK)
-            first_layer_pass(b, 0, 1)
-            for t in range(1, PACK):
-                for g in range(PASSES):
-                    first_layer_pass(b, t, g)
+            for t in range(PACK):
+                first_layer_pass(b, t, 1)
             h_grouped = keep.tile([P, BLOCK, PACK], BF16, name=f"h_grouped{b}", tag=f"h_grouped{b}", align_bytes=64)
-            nc.scalar.activation(out=h_grouped[:], in_=hidden[b][:].rearrange("p t j -> p j t"), func=ACT.Relu)
+            sums = hidden[b][:].rearrange("p t j -> p j t")
+            if b != VECTOR_RELU_BLOCK:
+                nc.scalar.activation(out=h_grouped[:], in_=sums, func=ACT.Relu)
+            else:
+                nc.vector.tensor_scalar_max(h_grouped[:], sums, 0.0)
             nc.vector.quantize_mx(
                 out=h_codes[:, cols].bitcast(FP8X4),
                 scales=h_scales[:, cols],
                 in_=h_grouped[:].rearrange("p j t -> p (j t)"),
             )
 
-        def head_columns(rows, w, t, cols, copy):
+        def head_columns(rows, w, t, runs, copy):
             acc = head_psum.tile([P, S], F32, name="acc")
-            nc.tensor.matmul_mx(
-                out=acc[:, cols],
-                lhsT=head_dealt[w][:, t * 2 * P : (t + 1) * 2 * P].bitcast(FP4X4),
-                lhsT_scale=head_scales[w][:, t * P : (t + 1) * P],
-                rhs=h_codes[:, cols].bitcast(FP8X4),
-                rhs_scale=h_scales[:, cols],
-                start=True,
-                stop=True,
-            )
+            for cols in runs:
+                nc.tensor.matmul_mx(
+                    out=acc[:, cols],
+                    lhsT=head_dealt[w][:, t * 2 * P : (t + 1) * 2 * P].bitcast(FP4X4),
+                    lhsT_scale=head_scales[w][:, t * P : (t + 1) * P],
+                    rhs=h_codes[:, cols].bitcast(FP8X4),
+                    rhs_scale=h_scales[:, cols],
+                    start=True,
+                    stop=True,
+                )
+            cols = slice(runs[0].start, runs[-1].stop)
             copy(out=rows[:, cols], in_=acc[:, cols])
 
         score = [keep.tile([P, S], F32, name=f"score{t}") for t in range(PACK)]
         feature = [keep.tile([P, S], F32, name=f"feature{t}") for t in range(PACK)]
 
         def make_score(t):
-            head_columns(score[t], 0, t, slice(0, S), nc.scalar.copy)
+            head_columns(score[t], 0, t, [slice(0, S)], nc.scalar.copy)
 
         def make_feature(t):
-            head_columns(feature[t], 1, t, slice(0, S), nc.scalar.copy)
+            head_columns(feature[t], 1, t, [slice(0, S)], nc.scalar.copy)
 
         def scratch(name, t):
             return keep.tile([P, V], F32, name=f"{name}{t}")
 
         pooled = keep.tile([P, PACK, V], F32)
         out_rows = out_0.rearrange("(p t) v -> p t v", t=PACK)
-        weight0 = [scratch("weight0_", 0)[:]] + [pooled[:, t, :] for t in range(PACK - 1)]
+        weight0 = [scratch("weight0_", t)[:] for t in range(PACK - 1)] + [pooled[:, PACK - 2, :]]
         weight1 = [scratch("weight1_", t) for t in range(PACK)]
         first_score = [scratch("first_score", t) for t in range(PACK)]
-        gap = [scratch("gap", t) for t in range(PACK)]
+        gap = [scratch("gap", 0)[:], scratch("gap", 1)[:], weight0[1], scratch("gap", 3)[:]]
         term0 = [scratch("term0_", t) for t in range(PACK)]
         term1 = [scratch("term1_", t) for t in range(PACK)]
         whole = slice(0, V)
@@ -212,17 +224,17 @@ def tile_picked_zrandla_relu_po_kernel(
         def entries(positions, part):
             return positions[:, part.start // 16 : part.stop // 16]
 
-        def score_gap(t):
-            for part in halves:
-                nc.vector.tensor_copy(first_score[t][:, part], score[t][:].indirect(entries(pos1_t, part)))
-            for part in halves:
-                nc.vector.tensor_tensor(
-                    gap[t][:, part], score[t][:].indirect(entries(pos2_t, part)), first_score[t][:, part], ALU.subtract
-                )
+        def fetch_first(t, part=whole):
+            nc.vector.tensor_copy(first_score[t][:, part], score[t][:].indirect(entries(pos1_t, part)))
+
+        def score_gap(t, part=whole):
+            nc.vector.tensor_tensor(
+                gap[t][:, part], score[t][:].indirect(entries(pos2_t, part)), first_score[t][:, part], ALU.subtract
+            )
 
         def make_weights(t):
-            nc.scalar.activation(out=weight0[t], in_=gap[t][:], func=ACT.Sigmoid, scale=-1.0)
-            nc.scalar.activation(out=weight1[t][:], in_=gap[t][:], func=ACT.Sigmoid)
+            nc.scalar.activation(out=weight0[t], in_=gap[t], func=ACT.Sigmoid, scale=-1.0)
+            nc.scalar.activation(out=weight1[t][:], in_=gap[t], func=ACT.Sigmoid)
 
         def weigh0(t):
             nc.vector.tensor_tensor(term0[t][:], feature[t][:].indirect(pos1_t[:]), weight0[t], ALU.mult)
@@ -238,27 +250,70 @@ def tile_picked_zrandla_relu_po_kernel(
         def pool(t, part):
             nc.vector.tensor_tensor(pooled[:, t, part], term0[t][:, part], term1[t][:, part], ALU.add)
 
+        turned = [keep.tile([P, 2, P], F32, name=f"turned{t}") for t in range(SUMMED_ON_TENSOR)]
+
+        def turn_sum(t):
+            turned_psum = hidden_psum.tile([P, 2, P], F32, name=f"hidden{2 * t % BLOCKS}")
+            for d, term in enumerate((term0[t], term1[t])):
+                for u in range(2):
+                    nc.tensor.matmul(
+                        turned_psum[:, u, :],
+                        lhsT=term[:, u * P : (u + 1) * P],
+                        rhs=identity[:],
+                        is_transpose=True,
+                        start=(d == 0 and u == 0),
+                        stop=(d == 1 and u == 1),
+                    )
+            nc.scalar.copy(out=turned[t][:], in_=turned_psum[:])
+
+        def turn_back(t):
+            back_psum = hidden_psum.tile([P, 2, P], F32, name=f"hidden{(2 * t + 1) % BLOCKS}")
+            for u in range(2):
+                nc.tensor.transpose(back_psum[:, u, :], turned[t][:, u, :], identity[:])
+            nc.scalar.copy(out=pooled[:, t, :], in_=back_psum[:].rearrange("p u v -> p (u v)"))
+
         def store(t):
             nc.sync.dma_start(out=out_rows[:, t, :], in_=pooled[:, t, :])
 
-        deal_scales(0, "h_grouped0")
-        head_columns(score[0], 0, 0, slice(0, S // 2), nc.vector.tensor_copy)
-        deal_scales(1, "h_grouped1")
-        head_columns(score[0], 0, 0, slice(2 * BLOCK, 3 * BLOCK), nc.vector.tensor_copy)
-        head_columns(score[0], 0, 0, slice(3 * BLOCK, S), nc.scalar.copy)
-        for t in range(1, PACK):
-            make_score(t)
-        for t in range(PACK):
-            score_gap(t)
-        for t in range(PACK):
-            make_feature(t)
-            make_weights(t)
-            weigh0(t)
-            if t >= 1:
-                pool(t - 1, whole)
-                store(t - 1)
-            if t + 1 < PACK:
-                weigh1(t, whole)
+        for cols in (slice(0, 2 * BLOCK), slice(3 * BLOCK, S), slice(2 * BLOCK, 3 * BLOCK)):
+            head_columns(score[0], 0, 0, [cols], nc.scalar.copy)
+        make_score(1)
+        deal_words(1, "h_grouped2")
+        deal_scales(1, "h_grouped3")
+        for t in range(2):
+            for part in halves:
+                fetch_first(t, part)
+            for part in halves:
+                score_gap(t, part)
+        make_feature(0)
+        make_weights(0)
+        weigh0(0)
+        weigh1(0, whole)
+        make_score(2)
+        fetch_first(2)
+        make_feature(1)
+        make_weights(1)
+        weigh0(1)
+        weigh1(1, whole)
+        score_gap(2)
+        make_score(3)
+        for part in halves:
+            fetch_first(3, part)
+        for part in halves:
+            score_gap(3, part)
+        make_feature(2)
+        turn_sum(0)
+        make_weights(2)
+        weigh0(2)
+        weigh1(2, whole)
+        turn_back(0)
+        store(0)
+        turn_sum(1)
+        make_feature(3)
+        make_weights(3)
+        weigh0(3)
+        turn_back(1)
+        store(1)
 
         out_grouped = keep.tile([P, V, PACK], BF16, align_bytes=64)
         out_codes = keep.tile([P, V], U32, align_bytes=64)
@@ -270,9 +325,12 @@ def tile_picked_zrandla_relu_po_kernel(
                 in_=pooled[:, first : first + 2, part].rearrange("p t v -> p v t"),
             )
 
-        round_pair(0, whole, nc.scalar.copy)
         for part in halves:
-            weigh1(PACK - 1, part)
+            round_pair(0, part, nc.scalar.copy)
+        weigh1(PACK - 1, halves[0])
+        pool(PACK - 2, whole)
+        store(PACK - 2)
+        weigh1(PACK - 1, halves[1])
         for part in halves:
             pool(PACK - 1, part)
         store(PACK - 1)

@@ -87,8 +87,8 @@ def tile_picked_zrandla_relu_po_kernel(
         def deal_words(w, tag):
             head_dealt[w] = keep.tile([P, 2 * N], U8, name=f"head_dealt{w}", tag=tag, align_bytes=64)
             nc.vector.tensor_copy(
-                out=head_dealt[w][:].rearrange("p (t m b) -> p t m b", t=PACK, b=2),
-                in_=head_words[w][:].rearrange("p (m t b) -> p t m b", t=PACK, b=2),
+                out=head_dealt[w][:].bitcast(U16).rearrange("p (t m) -> p t m", t=PACK),
+                in_=head_words[w][:].bitcast(U16).rearrange("p (m t) -> p t m", t=PACK),
             )
 
         def deal_scales(w, tag):
@@ -127,7 +127,7 @@ def tile_picked_zrandla_relu_po_kernel(
 
         low_tiles, high_tiles = slice(0, 2), slice(2, PACK)
         round_w1(0, low_tiles, 0, P, nc.scalar.copy)
-        round_w1(0, high_tiles, 0, P, nc.scalar.copy)
+        round_w1(0, high_tiles, 0, P, nc.vector.tensor_copy)
         round_w1(1, high_tiles, 0, P, nc.scalar.copy)
 
         hidden = [hidden_psum.tile([P, PACK, BLOCK], F32, name=f"hidden{b}") for b in range(BLOCKS)]
@@ -150,15 +150,15 @@ def tile_picked_zrandla_relu_po_kernel(
                 lhsT_scale=w1_scales[g][:, t * P : (t + 1) * P],
                 rhs=x_picked[g][:, cols].bitcast(FP8X4),
                 rhs_scale=x_scales_picked[4 * g : P, cols],
-                start=(g == 0 and t == 0),
+                start=(g == 0 and t == 2),
                 stop=(g == PASSES - 1 and t == PACK - 1),
             )
 
+        quantize_w1(0, high_tiles)
         pick_words(0, 0, S)
         quantize_w1(0, low_tiles)
-        quantize_w1(0, high_tiles)
         deal_scales(0, "head_scales0")
-        for t in range(PACK):
+        for t in (2, 3, 0, 1):
             for b in range(BLOCKS):
                 first_layer_pass(b, t, 0)
         round_w1(1, low_tiles, 0, P, nc.vector.tensor_copy)
@@ -303,13 +303,13 @@ def tile_picked_zrandla_relu_po_kernel(
             score_gap(3, part)
         make_feature(2)
         turn_sum(0)
+        make_feature(3)
         make_weights(2)
         weigh0(2)
         weigh1(2, whole)
         turn_back(0)
         store(0)
         turn_sum(1)
-        make_feature(3)
         make_weights(3)
         weigh0(3)
         turn_back(1)

@@ -22,7 +22,6 @@ PACK = 4
 PASSES = K // (P * PACK)
 BLOCK = 128
 BLOCKS = S // BLOCK
-VECTOR_RELU_BLOCK = 3
 QUADRANT_ORDER = (0, 2, 1, 3)
 SUMMED_ON_TENSOR = 2
 
@@ -34,10 +33,14 @@ def tile_picked_zrandla_relu_po_kernel(
     with ExitStack() as ctx:
         lists = ctx.enter_context(tc.tile_pool(name="lists", bufs=1))
         keep = ctx.enter_context(tc.tile_pool(name="keep", bufs=1))
+        shared = ctx.enter_context(tc.tile_pool(name="shared", bufs=1))
         hidden_psum = ctx.enter_context(tc.psum_pool(name="hidden_psum", bufs=1))
         head_psum = ctx.enter_context(tc.psum_pool(name="head_psum", bufs=4))
 
-        head_words = [keep.tile([P, 2 * N], U8, name=f"head_words{w}", align_bytes=64) for w in range(2)]
+        head_words = [
+            shared.tile([P, 2 * N], U8, name="head_words0", align_bytes=64, offset=256),
+            keep.tile([P, 2 * N], U8, name="head_words1", align_bytes=64),
+        ]
         x_scale_rows = keep.tile([P, T], U8, align_bytes=64)
         warm = keep.tile([P, 2], F32)
         nc.vector.memset(warm[:, 0:1], 0.0)
@@ -55,13 +58,13 @@ def tile_picked_zrandla_relu_po_kernel(
         pos1_t = lists.tile([P, V // 16], U16)
         pos2_t = lists.tile([P, V // 16], U16)
 
-        nc.sync.dma_start(out=head_words[0][:].bitcast(I32), in_=w2_words[0].bitcast(I32))
-        nc.sync.dma_start(offs_t[:], offs)
         for q in QUADRANT_ORDER:
             nc.sync.dma_start(
                 out=x_scale_landing[32 * q : 32 * q + 4 * PASSES, :],
                 in_=x_scales[:, 4 * q : 4 * q + 4, :].bitcast(I32),
             )
+        nc.sync.dma_start(offs_t[:], offs)
+
         def load_head_scales(w, scales, queue, quadrants):
             for q in quadrants:
                 queue.dma_start(
@@ -74,6 +77,7 @@ def tile_picked_zrandla_relu_po_kernel(
             nc.sync.dma_start(out=x_window[g][:], in_=x_words[g].rearrange("p n t -> p (n t)").bitcast(I32))
             if g == 0:
                 load_head_scales(0, w2_scales, nc.sync, QUADRANT_ORDER)
+        nc.sync.dma_start(out=head_words[0][:].bitcast(I32), in_=w2_words[0].bitcast(I32))
         nc.sync.dma_start(out=head_words[1][:].bitcast(I32), in_=w3_words[0].bitcast(I32))
         load_head_scales(1, w3_scales, nc.sync, QUADRANT_ORDER)
         nc.sync.dma_start(pos1_t[:], pos1)
@@ -98,7 +102,6 @@ def tile_picked_zrandla_relu_po_kernel(
                 in_=head_scale_rows[w][:].rearrange("p (m t) -> p t m", t=PACK),
             )
 
-        deal_words(0, "head_dealt0")
         for q in range(4):
             live = slice(32 * q, 32 * q + 4 * PASSES)
             nc.vector.tensor_copy(out=x_scale_rows[live, :].bitcast(I32), in_=x_scale_landing[live, :])
@@ -140,7 +143,7 @@ def tile_picked_zrandla_relu_po_kernel(
             )
 
         h_codes = keep.tile([P, S], U32, align_bytes=64)
-        h_scales = keep.tile([P, S], U8, align_bytes=64)
+        h_scales = shared.tile([P, S], U8, align_bytes=64, offset=0)
 
         def first_layer_pass(b, t, g):
             cols = slice(b * BLOCK, (b + 1) * BLOCK)
@@ -155,33 +158,44 @@ def tile_picked_zrandla_relu_po_kernel(
             )
 
         quantize_w1(0, high_tiles)
-        pick_words(0, 0, S)
+        pick_words(0, 0, S // 2)
         quantize_w1(0, low_tiles)
+        pick_words(0, S // 2, S)
         deal_scales(0, "head_scales0")
-        for t in (2, 3, 0, 1):
-            for b in range(BLOCKS):
-                first_layer_pass(b, t, 0)
+        for blocks in ((0, 1), (2, 3)):
+            for t in (2, 3, 0, 1):
+                for b in blocks:
+                    first_layer_pass(b, t, 0)
         round_w1(1, low_tiles, 0, P, nc.vector.tensor_copy)
         quantize_w1(1, low_tiles)
         pick_words(1, 0, BLOCK)
         quantize_w1(1, high_tiles)
         for b in range(1, BLOCKS):
             pick_words(1, b * BLOCK, (b + 1) * BLOCK)
-        for b in range(BLOCKS):
-            cols = slice(b * BLOCK, (b + 1) * BLOCK)
+        deal_words(0, "head_dealt0")
+        h_grouped = [
+            keep.tile([P, BLOCK, PACK], BF16, name=f"h_grouped{b}", tag=f"h_grouped{b}", align_bytes=64)
+            for b in range(BLOCKS - 1)
+        ] + [shared.tile([P, BLOCK, PACK], BF16, name="h_grouped_last", align_bytes=64, offset=512)]
+        def block_sums(b):
             for t in range(PACK):
                 first_layer_pass(b, t, 1)
-            h_grouped = keep.tile([P, BLOCK, PACK], BF16, name=f"h_grouped{b}", tag=f"h_grouped{b}", align_bytes=64)
-            sums = hidden[b][:].rearrange("p t j -> p j t")
-            if b != VECTOR_RELU_BLOCK:
-                nc.scalar.activation(out=h_grouped[:], in_=sums, func=ACT.Relu)
-            else:
-                nc.vector.tensor_scalar_max(h_grouped[:], sums, 0.0)
+            return hidden[b][:].rearrange("p t j -> p j t")
+
+        def quantize_h(b):
+            cols = slice(b * BLOCK, (b + 1) * BLOCK)
             nc.vector.quantize_mx(
                 out=h_codes[:, cols].bitcast(FP8X4),
                 scales=h_scales[:, cols],
-                in_=h_grouped[:].rearrange("p j t -> p (j t)"),
+                in_=h_grouped[b][:].rearrange("p j t -> p (j t)"),
             )
+
+        for b in range(BLOCKS - 1):
+            nc.scalar.activation(out=h_grouped[b][:], in_=block_sums(b), func=ACT.Relu)
+        quantize_h(0)
+        nc.vector.tensor_scalar_max(h_grouped[3][:], block_sums(3), 0.0)
+        for b in (1, 3, 2):
+            quantize_h(b)
 
         def head_columns(rows, w, t, runs, copy):
             acc = head_psum.tile([P, S], F32, name="acc")
@@ -278,8 +292,8 @@ def tile_picked_zrandla_relu_po_kernel(
         for cols in (slice(0, 2 * BLOCK), slice(3 * BLOCK, S), slice(2 * BLOCK, 3 * BLOCK)):
             head_columns(score[0], 0, 0, [cols], nc.scalar.copy)
         make_score(1)
-        deal_words(1, "h_grouped2")
-        deal_scales(1, "h_grouped3")
+        deal_words(1, "h_grouped1")
+        deal_scales(1, "h_grouped2")
         for t in range(2):
             for part in halves:
                 fetch_first(t, part)

@@ -20,10 +20,20 @@ ALU = mybir.AluOpType
 P = 128
 PACK = 4
 PASSES = K // (P * PACK)
-BLOCK = 128
-BLOCKS = S // BLOCK
+BATCH = 128
+BATCHES = S // BATCH
+QUADRANT = 32
+ENTRIES_PER_COLUMN = 16
 QUADRANT_ORDER = (0, 2, 1, 3)
+SCORES, FEATURES = 0, 1
 SUMMED_ON_TENSOR = 2
+
+H_SCALES_AT = 0
+SCORE_WORDS_RAW_AT = 256
+VECTOR_BATCH_AT = 512
+LAST_BATCH_AT = 2048
+FEATURE_SCALES_AT = LAST_BATCH_AT
+FEATURE_WORDS_AT = LAST_BATCH_AT + N
 
 
 def tile_picked_zrandla_relu_po_kernel(
@@ -33,193 +43,210 @@ def tile_picked_zrandla_relu_po_kernel(
     with ExitStack() as ctx:
         lists = ctx.enter_context(tc.tile_pool(name="lists", bufs=1))
         keep = ctx.enter_context(tc.tile_pool(name="keep", bufs=1))
-        shared = ctx.enter_context(tc.tile_pool(name="shared", bufs=1))
+        reused = ctx.enter_context(tc.tile_pool(name="reused", bufs=1))
         hidden_psum = ctx.enter_context(tc.psum_pool(name="hidden_psum", bufs=1))
         head_psum = ctx.enter_context(tc.psum_pool(name="head_psum", bufs=4))
 
-        head_words = [
-            shared.tile([P, 2 * N], U8, name="head_words0", align_bytes=64, offset=256),
-            keep.tile([P, 2 * N], U8, name="head_words1", align_bytes=64),
+        head_words_raw = [
+            reused.tile([P, 2 * N], U8, name="score_words_raw", align_bytes=64, offset=SCORE_WORDS_RAW_AT),
+            keep.tile([P, 2 * N], U8, name="feature_words_raw", align_bytes=64),
         ]
-        x_scale_rows = keep.tile([P, T], U8, align_bytes=64)
+        x_scale_window = keep.tile([P, T], U8, align_bytes=64)
         warm = keep.tile([P, 2], F32)
         nc.vector.memset(warm[:, 0:1], 0.0)
         nc.scalar.activation(out=warm[:, 1:2], in_=warm[:, 0:1], func=ACT.Sigmoid)
-        head_scale_rows = [keep.tile([P, N], U8, name=f"head_scale_rows{w}", align_bytes=64) for w in range(2)]
-        nc.vector.memset(head_scale_rows[0][:].bitcast(I32), 0)
-        nc.gpsimd.memset(x_scale_rows[:].bitcast(I32), 0)
-        nc.gpsimd.memset(head_scale_rows[1][:].bitcast(I32), 0)
+        head_scales_raw = [keep.tile([P, N], U8, name=f"head_scales_raw{w}", align_bytes=64) for w in range(2)]
+        nc.vector.memset(head_scales_raw[SCORES][:].bitcast(I32), 0)
+        nc.gpsimd.memset(x_scale_window[:].bitcast(I32), 0)
+        nc.gpsimd.memset(head_scales_raw[FEATURES][:].bitcast(I32), 0)
 
         w1_raw = [keep.tile([P, PACK, H], F32, name=f"w1_raw{g}", align_bytes=64) for g in range(PASSES)]
         w1_rows = w1.rearrange("(g p j) c -> g p j c", p=P, j=PACK)
         x_window = [keep.tile([P, T], I32, name=f"x_window{g}", align_bytes=64) for g in range(PASSES)]
         x_scale_landing = keep.tile([P, T // 4], I32)
-        offs_t = lists.tile([P, S // 16], U16)
-        pos1_t = lists.tile([P, V // 16], U16)
-        pos2_t = lists.tile([P, V // 16], U16)
+        offs_t = lists.tile([P, S // ENTRIES_PER_COLUMN], U16)
+        pos1_t = lists.tile([P, V // ENTRIES_PER_COLUMN], U16)
+        pos2_t = lists.tile([P, V // ENTRIES_PER_COLUMN], U16)
 
         for q in QUADRANT_ORDER:
             nc.sync.dma_start(
-                out=x_scale_landing[32 * q : 32 * q + 4 * PASSES, :],
+                out=x_scale_landing[QUADRANT * q : QUADRANT * q + 4 * PASSES, :],
                 in_=x_scales[:, 4 * q : 4 * q + 4, :].bitcast(I32),
             )
         nc.sync.dma_start(offs_t[:], offs)
 
-        def load_head_scales(w, scales, queue, quadrants):
-            for q in quadrants:
-                queue.dma_start(
-                    out=head_scale_rows[w][32 * q : 32 * q + 4, :].bitcast(I32),
+        def load_head_scales(w, scales):
+            for q in QUADRANT_ORDER:
+                nc.sync.dma_start(
+                    out=head_scales_raw[w][QUADRANT * q : QUADRANT * q + 4, :].bitcast(I32),
                     in_=scales[0, 4 * q : 4 * q + 4, :].bitcast(I32),
                 )
 
-        for g in range(PASSES):
+        def load_pass(g):
             nc.sync.dma_start(out=w1_raw[g][:], in_=w1_rows[g])
             nc.sync.dma_start(out=x_window[g][:], in_=x_words[g].rearrange("p n t -> p (n t)").bitcast(I32))
-            if g == 0:
-                load_head_scales(0, w2_scales, nc.sync, QUADRANT_ORDER)
-        nc.sync.dma_start(out=head_words[0][:].bitcast(I32), in_=w2_words[0].bitcast(I32))
-        nc.sync.dma_start(out=head_words[1][:].bitcast(I32), in_=w3_words[0].bitcast(I32))
-        load_head_scales(1, w3_scales, nc.sync, QUADRANT_ORDER)
+
+        load_pass(0)
+        load_head_scales(SCORES, w2_scales)
+        load_pass(1)
+        nc.sync.dma_start(out=head_words_raw[SCORES][:].bitcast(I32), in_=w2_words[0].bitcast(I32))
+        nc.sync.dma_start(out=head_words_raw[FEATURES][:].bitcast(I32), in_=w3_words[0].bitcast(I32))
+        load_head_scales(FEATURES, w3_scales)
         nc.sync.dma_start(pos1_t[:], pos1)
         nc.sync.dma_start(pos2_t[:], pos2)
         identity = keep.tile([P, P], F32)
         make_identity(nc, identity[:])
 
-        head_dealt = [None, None]
-        head_scales = [None, None]
-
-        def deal_words(w, tag):
-            head_dealt[w] = keep.tile([P, 2 * N], U8, name=f"head_dealt{w}", tag=tag, align_bytes=64)
+        def deal_words(w, dealt):
             nc.vector.tensor_copy(
-                out=head_dealt[w][:].bitcast(U16).rearrange("p (t m) -> p t m", t=PACK),
-                in_=head_words[w][:].bitcast(U16).rearrange("p (m t) -> p t m", t=PACK),
+                out=dealt[:].bitcast(U16).rearrange("p (t c) -> p t c", t=PACK),
+                in_=head_words_raw[w][:].bitcast(U16).rearrange("p (c t) -> p t c", t=PACK),
             )
 
-        def deal_scales(w, tag):
-            head_scales[w] = keep.tile([P, N], U8, name=f"head_scales{w}", tag=tag, align_bytes=64)
+        def deal_scales(w, dealt):
             nc.vector.tensor_copy(
-                out=head_scales[w][:].rearrange("p (t m) -> p t m", t=PACK),
-                in_=head_scale_rows[w][:].rearrange("p (m t) -> p t m", t=PACK),
+                out=dealt[:].rearrange("p (t c) -> p t c", t=PACK),
+                in_=head_scales_raw[w][:].rearrange("p (c t) -> p t c", t=PACK),
             )
 
-        for q in range(4):
-            live = slice(32 * q, 32 * q + 4 * PASSES)
-            nc.vector.tensor_copy(out=x_scale_rows[live, :].bitcast(I32), in_=x_scale_landing[live, :])
+        for q in range(P // QUADRANT):
+            live = slice(QUADRANT * q, QUADRANT * q + 4 * PASSES)
+            nc.vector.tensor_copy(out=x_scale_window[live, :].bitcast(I32), in_=x_scale_landing[live, :])
         x_scales_picked = keep.tile([P, S], U8, align_bytes=64)
-        nc.vector.tensor_copy(x_scales_picked[:], x_scale_rows[:].indirect(offs_t[:]))
+        nc.vector.tensor_copy(x_scales_picked[:], x_scale_window[:].indirect(offs_t[:]))
 
         w1_grouped = [keep.tile([P, PACK, P, PACK], BF16, name=f"w1_grouped{g}", align_bytes=64) for g in range(PASSES)]
         w1_codes = [keep.tile([P, H], U32, name=f"w1_codes{g}", align_bytes=64) for g in range(PASSES)]
         w1_scales = [keep.tile([P, H], U8, name=f"w1_scales{g}", align_bytes=64) for g in range(PASSES)]
 
-        def round_w1(g, tiles, first, last, copy):
+        def round_w1(g, tiles, part, copy):
             copy(
-                out=w1_grouped[g][:, tiles, first:last, :].rearrange("p t m j -> p m j t"),
-                in_=w1_raw[g][:, :, PACK * first : PACK * last].rearrange("p j (m t) -> p m j t", t=PACK)[
+                out=w1_grouped[g][:, tiles, part, :].rearrange("p t c j -> p c j t"),
+                in_=w1_raw[g][:, :, PACK * part.start : PACK * part.stop].rearrange("p j (c t) -> p c j t", t=PACK)[
                     :, :, :, tiles
                 ],
             )
 
-        def quantize_w1(g, tiles):
-            cols = slice(tiles.start * P, tiles.stop * P)
+        def quantize_w1(g, cols):
             nc.vector.quantize_mx(
                 out=w1_codes[g][:, cols].bitcast(FP8X4),
                 scales=w1_scales[g][:, cols],
-                in_=w1_grouped[g][:, tiles].rearrange("p t m j -> p (t m j)"),
+                in_=w1_grouped[g][:].rearrange("p t c j -> p (t c j)")[:, PACK * cols.start : PACK * cols.stop],
             )
 
         low_tiles, high_tiles = slice(0, 2), slice(2, PACK)
-        round_w1(0, low_tiles, 0, P, nc.scalar.copy)
-        round_w1(0, high_tiles, 0, P, nc.vector.tensor_copy)
-        round_w1(1, high_tiles, 0, P, nc.scalar.copy)
+        low_cols, high_cols = slice(0, 2 * P), slice(2 * P, H)
+        tile_whole = slice(0, P)
+        tile_halves = (slice(0, P // 2), slice(P // 2, P))
+        round_w1(0, low_tiles, tile_whole, nc.scalar.copy)
+        round_w1(0, high_tiles, tile_whole, nc.vector.tensor_copy)
+        round_w1(1, high_tiles, tile_whole, nc.scalar.copy)
 
-        hidden = [hidden_psum.tile([P, PACK, BLOCK], F32, name=f"hidden{b}") for b in range(BLOCKS)]
+        hidden = [hidden_psum.tile([P, PACK, BATCH], F32, name=f"hidden{b}") for b in range(BATCHES)]
         x_picked = [keep.tile([P, S], U32, name=f"x_picked{g}", align_bytes=64) for g in range(PASSES)]
 
-        def pick_words(g, first, last):
-            nc.vector.tensor_copy(
-                x_picked[g][:, first:last],
-                x_window[g][:].bitcast(U32).indirect(offs_t[:, first // 16 : last // 16]),
-            )
+        def entries(list_tile, part):
+            return list_tile[:, part.start // ENTRIES_PER_COLUMN : part.stop // ENTRIES_PER_COLUMN]
+
+        def batch_cols(b):
+            return slice(b * BATCH, (b + 1) * BATCH)
+
+        def pick_words(g, part):
+            nc.vector.tensor_copy(x_picked[g][:, part], x_window[g][:].bitcast(U32).indirect(entries(offs_t, part)))
 
         h_codes = keep.tile([P, S], U32, align_bytes=64)
-        h_scales = shared.tile([P, S], U8, align_bytes=64, offset=0)
+        h_scales = reused.tile([P, S], U8, align_bytes=64, offset=H_SCALES_AT)
+
+        first_pass_tiles = (2, 3, 0, 1)
 
         def first_layer_pass(b, t, g):
-            cols = slice(b * BLOCK, (b + 1) * BLOCK)
             nc.tensor.matmul_mx(
                 out=hidden[b][:, t, :],
                 lhsT=w1_codes[g][:, t * P : (t + 1) * P].bitcast(FP8X4),
                 lhsT_scale=w1_scales[g][:, t * P : (t + 1) * P],
-                rhs=x_picked[g][:, cols].bitcast(FP8X4),
-                rhs_scale=x_scales_picked[4 * g : P, cols],
-                start=(g == 0 and t == 2),
+                rhs=x_picked[g][:, batch_cols(b)].bitcast(FP8X4),
+                rhs_scale=x_scales_picked[4 * g : P, batch_cols(b)],
+                start=(g == 0 and t == first_pass_tiles[0]),
                 stop=(g == PASSES - 1 and t == PACK - 1),
             )
 
-        quantize_w1(0, high_tiles)
-        pick_words(0, 0, S // 2)
-        quantize_w1(0, low_tiles)
-        pick_words(0, S // 2, S)
-        deal_scales(0, "head_scales0")
-        for blocks in ((0, 1), (2, 3)):
-            for t in (2, 3, 0, 1):
-                for b in blocks:
+        quantize_w1(0, high_cols)
+        pick_words(0, slice(0, S // 2))
+        quantize_w1(0, low_cols)
+        pick_words(0, slice(S // 2, S))
+        score_scales = keep.tile([P, N], U8, align_bytes=64)
+        deal_scales(SCORES, score_scales)
+        for batches in ((0, 1), (2, 3)):
+            for t in first_pass_tiles:
+                for b in batches:
                     first_layer_pass(b, t, 0)
-        round_w1(1, low_tiles, 0, P, nc.vector.tensor_copy)
-        quantize_w1(1, low_tiles)
-        pick_words(1, 0, BLOCK)
-        quantize_w1(1, high_tiles)
-        for b in range(1, BLOCKS):
-            pick_words(1, b * BLOCK, (b + 1) * BLOCK)
-        deal_words(0, "head_dealt0")
-        h_grouped = [
-            keep.tile([P, BLOCK, PACK], BF16, name=f"h_grouped{b}", tag=f"h_grouped{b}", align_bytes=64)
-            for b in range(BLOCKS - 1)
-        ] + [shared.tile([P, BLOCK, PACK], BF16, name="h_grouped_last", align_bytes=64, offset=512)]
-        def block_sums(b):
+        for part in tile_halves:
+            round_w1(1, low_tiles, part, nc.vector.tensor_copy)
+        for part in tile_halves:
+            for t in range(low_tiles.start, low_tiles.stop):
+                quantize_w1(1, slice(t * P + part.start, t * P + part.stop))
+        pick_words(1, batch_cols(0))
+        quantize_w1(1, high_cols)
+        for b in range(1, BATCHES):
+            pick_words(1, batch_cols(b))
+        score_words = keep.tile([P, 2 * N], U8, align_bytes=64)
+        deal_words(SCORES, score_words)
+
+        h_grouped = [keep.tile([P, BATCH, PACK], BF16, name=f"h_grouped{b}", align_bytes=64) for b in range(2)] + [
+            reused.tile([P, BATCH, PACK], BF16, name="h_grouped2", align_bytes=64, offset=LAST_BATCH_AT),
+            reused.tile([P, BATCH, PACK], BF16, name="h_grouped3", align_bytes=64, offset=VECTOR_BATCH_AT),
+        ]
+        batch_whole = slice(0, BATCH)
+        batch_halves = (slice(0, BATCH // 2), slice(BATCH // 2, BATCH))
+
+        def close_batch(b):
             for t in range(PACK):
                 first_layer_pass(b, t, 1)
-            return hidden[b][:].rearrange("p t j -> p j t")
+            return hidden[b][:].rearrange("p t e -> p e t")
 
-        def quantize_h(b):
-            cols = slice(b * BLOCK, (b + 1) * BLOCK)
+        def quantize_h(b, part):
+            cols = slice(b * BATCH + part.start, b * BATCH + part.stop)
             nc.vector.quantize_mx(
                 out=h_codes[:, cols].bitcast(FP8X4),
                 scales=h_scales[:, cols],
-                in_=h_grouped[b][:].rearrange("p j t -> p (j t)"),
+                in_=h_grouped[b][:, part, :].rearrange("p e t -> p (e t)"),
             )
 
-        for b in range(BLOCKS - 1):
-            nc.scalar.activation(out=h_grouped[b][:], in_=block_sums(b), func=ACT.Relu)
-        quantize_h(0)
-        nc.vector.tensor_scalar_max(h_grouped[3][:], block_sums(3), 0.0)
-        for b in (1, 3, 2):
-            quantize_h(b)
+        for b in range(2):
+            nc.scalar.activation(out=h_grouped[b][:], in_=close_batch(b), func=ACT.Relu)
+        last_sums = close_batch(2)
+        for part in batch_halves:
+            nc.scalar.activation(out=h_grouped[2][:, part, :], in_=last_sums[:, part, :], func=ACT.Relu)
+        quantize_h(0, batch_whole)
+        nc.vector.tensor_scalar_max(h_grouped[3][:], close_batch(3), 0.0)
+        quantize_h(1, batch_whole)
+        quantize_h(3, batch_whole)
+        for part in batch_halves:
+            quantize_h(2, part)
 
-        def head_columns(rows, w, t, runs, copy):
+        def head_columns(rows, words, scales, t, cols):
             acc = head_psum.tile([P, S], F32, name="acc")
-            for cols in runs:
-                nc.tensor.matmul_mx(
-                    out=acc[:, cols],
-                    lhsT=head_dealt[w][:, t * 2 * P : (t + 1) * 2 * P].bitcast(FP4X4),
-                    lhsT_scale=head_scales[w][:, t * P : (t + 1) * P],
-                    rhs=h_codes[:, cols].bitcast(FP8X4),
-                    rhs_scale=h_scales[:, cols],
-                    start=True,
-                    stop=True,
-                )
-            cols = slice(runs[0].start, runs[-1].stop)
-            copy(out=rows[:, cols], in_=acc[:, cols])
+            nc.tensor.matmul_mx(
+                out=acc[:, cols],
+                lhsT=words[:, t * 2 * P : (t + 1) * 2 * P].bitcast(FP4X4),
+                lhsT_scale=scales[:, t * P : (t + 1) * P],
+                rhs=h_codes[:, cols].bitcast(FP8X4),
+                rhs_scale=h_scales[:, cols],
+                start=True,
+                stop=True,
+            )
+            nc.scalar.copy(out=rows[:, cols], in_=acc[:, cols])
 
         score = [keep.tile([P, S], F32, name=f"score{t}") for t in range(PACK)]
         feature = [keep.tile([P, S], F32, name=f"feature{t}") for t in range(PACK)]
+        feature_words = reused.tile([P, 2 * N], U8, align_bytes=64, offset=FEATURE_WORDS_AT)
+        feature_scales = reused.tile([P, N], U8, align_bytes=64, offset=FEATURE_SCALES_AT)
 
         def make_score(t):
-            head_columns(score[t], 0, t, [slice(0, S)], nc.scalar.copy)
+            head_columns(score[t], score_words, score_scales, t, slice(0, S))
 
         def make_feature(t):
-            head_columns(feature[t], 1, t, [slice(0, S)], nc.scalar.copy)
+            head_columns(feature[t], feature_words, feature_scales, t, slice(0, S))
 
         def scratch(name, t):
             return keep.tile([P, V], F32, name=f"{name}{t}")
@@ -232,19 +259,22 @@ def tile_picked_zrandla_relu_po_kernel(
         gap = [scratch("gap", 0)[:], scratch("gap", 1)[:], weight0[1], scratch("gap", 3)[:]]
         term0 = [scratch("term0_", t) for t in range(PACK)]
         term1 = [scratch("term1_", t) for t in range(PACK)]
-        whole = slice(0, V)
-        halves = (slice(0, V // 2), slice(V // 2, V))
+        centres = slice(0, V)
+        centre_halves = (slice(0, V // 2), slice(V // 2, V))
 
-        def entries(positions, part):
-            return positions[:, part.start // 16 : part.stop // 16]
-
-        def fetch_first(t, part=whole):
+        def fetch_first(t, part):
             nc.vector.tensor_copy(first_score[t][:, part], score[t][:].indirect(entries(pos1_t, part)))
 
-        def score_gap(t, part=whole):
+        def score_gap(t, part):
             nc.vector.tensor_tensor(
                 gap[t][:, part], score[t][:].indirect(entries(pos2_t, part)), first_score[t][:, part], ALU.subtract
             )
+
+        def gap_by_halves(t):
+            for part in centre_halves:
+                fetch_first(t, part)
+            for part in centre_halves:
+                score_gap(t, part)
 
         def make_weights(t):
             nc.scalar.activation(out=weight0[t], in_=gap[t], func=ACT.Sigmoid, scale=-1.0)
@@ -255,19 +285,16 @@ def tile_picked_zrandla_relu_po_kernel(
 
         def weigh1(t, part):
             nc.vector.tensor_tensor(
-                term1[t][:, part],
-                feature[t][:].indirect(pos2_t[:, part.start // 16 : part.stop // 16]),
-                weight1[t][:, part],
-                ALU.mult,
+                term1[t][:, part], feature[t][:].indirect(entries(pos2_t, part)), weight1[t][:, part], ALU.mult
             )
 
-        def pool(t, part):
+        def add_terms(t, part):
             nc.vector.tensor_tensor(pooled[:, t, part], term0[t][:, part], term1[t][:, part], ALU.add)
 
         turned = [keep.tile([P, 2, P], F32, name=f"turned{t}") for t in range(SUMMED_ON_TENSOR)]
 
         def turn_sum(t):
-            turned_psum = hidden_psum.tile([P, 2, P], F32, name=f"hidden{2 * t % BLOCKS}")
+            turned_psum = hidden_psum.tile([P, 2, P], F32, name=f"hidden{2 * t}")
             for d, term in enumerate((term0[t], term1[t])):
                 for u in range(2):
                     nc.tensor.matmul(
@@ -281,7 +308,7 @@ def tile_picked_zrandla_relu_po_kernel(
             nc.scalar.copy(out=turned[t][:], in_=turned_psum[:])
 
         def turn_back(t):
-            back_psum = hidden_psum.tile([P, 2, P], F32, name=f"hidden{(2 * t + 1) % BLOCKS}")
+            back_psum = hidden_psum.tile([P, 2, P], F32, name=f"hidden{2 * t + 1}")
             for u in range(2):
                 nc.tensor.transpose(back_psum[:, u, :], turned[t][:, u, :], identity[:])
             nc.scalar.copy(out=pooled[:, t, :], in_=back_psum[:].rearrange("p u v -> p (u v)"))
@@ -289,38 +316,32 @@ def tile_picked_zrandla_relu_po_kernel(
         def store(t):
             nc.sync.dma_start(out=out_rows[:, t, :], in_=pooled[:, t, :])
 
-        for cols in (slice(0, 2 * BLOCK), slice(3 * BLOCK, S), slice(2 * BLOCK, 3 * BLOCK)):
-            head_columns(score[0], 0, 0, [cols], nc.scalar.copy)
+        for b in (0, 1, 3, 2):
+            head_columns(score[0], score_words, score_scales, 0, batch_cols(b))
         make_score(1)
-        deal_words(1, "h_grouped1")
-        deal_scales(1, "h_grouped2")
-        for t in range(2):
-            for part in halves:
-                fetch_first(t, part)
-            for part in halves:
-                score_gap(t, part)
+        deal_words(FEATURES, feature_words)
+        deal_scales(FEATURES, feature_scales)
+        gap_by_halves(0)
+        gap_by_halves(1)
         make_feature(0)
         make_weights(0)
         weigh0(0)
-        weigh1(0, whole)
+        weigh1(0, centres)
         make_score(2)
-        fetch_first(2)
+        fetch_first(2, centres)
         make_feature(1)
         make_weights(1)
         weigh0(1)
-        weigh1(1, whole)
-        score_gap(2)
+        weigh1(1, centres)
+        score_gap(2, centres)
         make_score(3)
-        for part in halves:
-            fetch_first(3, part)
-        for part in halves:
-            score_gap(3, part)
+        gap_by_halves(3)
         make_feature(2)
         turn_sum(0)
         make_feature(3)
         make_weights(2)
         weigh0(2)
-        weigh1(2, whole)
+        weigh1(2, centres)
         turn_back(0)
         store(0)
         turn_sum(1)
@@ -333,33 +354,30 @@ def tile_picked_zrandla_relu_po_kernel(
         out_codes = keep.tile([P, V], U32, align_bytes=64)
         out_scales = keep.tile([P, V], U8, align_bytes=64)
 
-        def round_pair(first, part, copy):
-            copy(
-                out=out_grouped[:, part, first : first + 2],
-                in_=pooled[:, first : first + 2, part].rearrange("p t v -> p v t"),
-            )
+        def round_pair(tiles, part, copy):
+            copy(out=out_grouped[:, part, tiles], in_=pooled[:, tiles, part].rearrange("p t v -> p v t"))
 
-        for part in halves:
-            round_pair(0, part, nc.scalar.copy)
-        weigh1(PACK - 1, halves[0])
-        pool(PACK - 2, whole)
-        store(PACK - 2)
-        weigh1(PACK - 1, halves[1])
-        for part in halves:
-            pool(PACK - 1, part)
-        store(PACK - 1)
-        for part in halves:
-            round_pair(2, part, nc.vector.tensor_copy)
-        for part in halves:
+        for part in centre_halves:
+            round_pair(low_tiles, part, nc.scalar.copy)
+        weigh1(3, centre_halves[0])
+        add_terms(2, centres)
+        store(2)
+        weigh1(3, centre_halves[1])
+        for part in centre_halves:
+            add_terms(3, part)
+        store(3)
+        for part in centre_halves:
+            round_pair(high_tiles, part, nc.vector.tensor_copy)
+        for part in centre_halves:
             nc.vector.quantize_mx(
                 out=out_codes[:, part].bitcast(FP8X4),
                 scales=out_scales[:, part],
                 in_=out_grouped[:, part, :].rearrange("p v t -> p (v t)"),
             )
         nc.sync.dma_start(out=out_1[0].rearrange("p c r -> p (c r)").bitcast(I32), in_=out_codes[:].bitcast(I32))
-        for q in range(4):
+        for q in range(P // QUADRANT):
             queue = nc.scalar if q % 2 else nc.sync
             queue.dma_start(
                 out=out_2[0, 4 * q : 4 * q + 4, :].bitcast(I32),
-                in_=out_scales[32 * q : 32 * q + 4, :].bitcast(I32),
+                in_=out_scales[QUADRANT * q : QUADRANT * q + 4, :].bitcast(I32),
             )

@@ -52,28 +52,31 @@ def tile_picked_zrandla_relu_po_kernel(
             keep.tile([P, 2 * N], U8, name="feature_words_raw", align_bytes=64),
         ]
         x_scale_window = keep.tile([P, T], U8, align_bytes=64)
+        nc.vector.memset(x_scale_window[:].bitcast(I32), 0)
         warm = keep.tile([P, 2], F32)
         nc.vector.memset(warm[:, 0:1], 0.0)
         nc.scalar.activation(out=warm[:, 1:2], in_=warm[:, 0:1], func=ACT.Sigmoid)
         head_scales_raw = [keep.tile([P, N], U8, name=f"head_scales_raw{w}", align_bytes=64) for w in range(2)]
-        nc.vector.memset(head_scales_raw[SCORES][:].bitcast(I32), 0)
-        nc.gpsimd.memset(x_scale_window[:].bitcast(I32), 0)
+        nc.gpsimd.memset(head_scales_raw[SCORES][:].bitcast(I32), 0)
         nc.gpsimd.memset(head_scales_raw[FEATURES][:].bitcast(I32), 0)
 
         w1_raw = [keep.tile([P, PACK, H], F32, name=f"w1_raw{g}", align_bytes=64) for g in range(PASSES)]
         w1_rows = w1.rearrange("(g p j) c -> g p j c", p=P, j=PACK)
         x_window = [keep.tile([P, T], I32, name=f"x_window{g}", align_bytes=64) for g in range(PASSES)]
-        x_scale_landing = keep.tile([P, T // 4], I32)
         offs_t = lists.tile([P, S // ENTRIES_PER_COLUMN], U16)
         pos1_t = lists.tile([P, V // ENTRIES_PER_COLUMN], U16)
         pos2_t = lists.tile([P, V // ENTRIES_PER_COLUMN], U16)
 
+        def load_x(g):
+            nc.sync.dma_start(out=x_window[g][:], in_=x_words[g].rearrange("p n t -> p (n t)").bitcast(I32))
+
+        load_x(0)
+        nc.sync.dma_start(offs_t[:], offs)
         for q in QUADRANT_ORDER:
             nc.sync.dma_start(
-                out=x_scale_landing[QUADRANT * q : QUADRANT * q + 4 * PASSES, :],
+                out=x_scale_window[QUADRANT * q : QUADRANT * q + 4 * PASSES, :].bitcast(I32),
                 in_=x_scales[:, 4 * q : 4 * q + 4, :].bitcast(I32),
             )
-        nc.sync.dma_start(offs_t[:], offs)
 
         def load_head_scales(w, scales):
             for q in QUADRANT_ORDER:
@@ -82,13 +85,10 @@ def tile_picked_zrandla_relu_po_kernel(
                     in_=scales[0, 4 * q : 4 * q + 4, :].bitcast(I32),
                 )
 
-        def load_pass(g):
-            nc.sync.dma_start(out=w1_raw[g][:], in_=w1_rows[g])
-            nc.sync.dma_start(out=x_window[g][:], in_=x_words[g].rearrange("p n t -> p (n t)").bitcast(I32))
-
-        load_pass(0)
+        nc.sync.dma_start(out=w1_raw[0][:], in_=w1_rows[0])
         load_head_scales(SCORES, w2_scales)
-        load_pass(1)
+        nc.sync.dma_start(out=w1_raw[1][:], in_=w1_rows[1])
+        load_x(1)
         nc.sync.dma_start(out=head_words_raw[SCORES][:].bitcast(I32), in_=w2_words[0].bitcast(I32))
         nc.sync.dma_start(out=head_words_raw[FEATURES][:].bitcast(I32), in_=w3_words[0].bitcast(I32))
         load_head_scales(FEATURES, w3_scales)
@@ -109,9 +109,8 @@ def tile_picked_zrandla_relu_po_kernel(
                 in_=head_scales_raw[w][:].rearrange("p (c t) -> p t c", t=PACK),
             )
 
-        for q in range(P // QUADRANT):
-            live = slice(QUADRANT * q, QUADRANT * q + 4 * PASSES)
-            nc.vector.tensor_copy(out=x_scale_window[live, :].bitcast(I32), in_=x_scale_landing[live, :])
+        x_picked = [keep.tile([P, S], U32, name=f"x_picked{g}", align_bytes=64) for g in range(PASSES)]
+        nc.vector.tensor_copy(x_picked[0][:], x_window[0][:].bitcast(U32).indirect(offs_t[:]))
         x_scales_picked = keep.tile([P, S], U8, align_bytes=64)
         nc.vector.tensor_copy(x_scales_picked[:], x_scale_window[:].indirect(offs_t[:]))
 
@@ -143,7 +142,6 @@ def tile_picked_zrandla_relu_po_kernel(
         round_w1(1, high_tiles, tile_whole, nc.scalar.copy)
 
         hidden = [hidden_psum.tile([P, PACK, BATCH], F32, name=f"hidden{b}") for b in range(BATCHES)]
-        x_picked = [keep.tile([P, S], U32, name=f"x_picked{g}", align_bytes=64) for g in range(PASSES)]
 
         def entries(list_tile, part):
             return list_tile[:, part.start // ENTRIES_PER_COLUMN : part.stop // ENTRIES_PER_COLUMN]
@@ -170,16 +168,13 @@ def tile_picked_zrandla_relu_po_kernel(
                 stop=(g == PASSES - 1 and t == PACK - 1),
             )
 
-        quantize_w1(0, high_cols)
-        pick_words(0, slice(0, S // 2))
-        quantize_w1(0, low_cols)
-        pick_words(0, slice(S // 2, S))
         score_scales = keep.tile([P, N], U8, align_bytes=64)
         deal_scales(SCORES, score_scales)
-        for batches in ((0, 1), (2, 3)):
-            for t in first_pass_tiles:
-                for b in batches:
-                    first_layer_pass(b, t, 0)
+        quantize_w1(0, high_cols)
+        quantize_w1(0, low_cols)
+        for t in first_pass_tiles:
+            for b in range(BATCHES):
+                first_layer_pass(b, t, 0)
         for part in tile_halves:
             round_w1(1, low_tiles, part, nc.vector.tensor_copy)
         for part in tile_halves:

@@ -57,8 +57,11 @@ def tile_picked_zrandla_relu_po_kernel(
         nc.vector.memset(warm[:, 0:1], 0.0)
         nc.scalar.activation(out=warm[:, 1:2], in_=warm[:, 0:1], func=ACT.Sigmoid)
         head_scales_raw = [keep.tile([P, N], U8, name=f"head_scales_raw{w}", align_bytes=64) for w in range(2)]
-        nc.gpsimd.memset(head_scales_raw[SCORES][:].bitcast(I32), 0)
-        nc.gpsimd.memset(head_scales_raw[FEATURES][:].bitcast(I32), 0)
+        nc.vector.memset(head_scales_raw[SCORES][:].bitcast(I32), 0)
+        nc.vector.memset(head_scales_raw[FEATURES][:].bitcast(I32), 0)
+        identity = keep.tile([P, P], F32)
+        nc.vector.memset(identity[:], 0.0)
+        make_identity(nc, identity[:], nomemset=True)
 
         w1_raw = [keep.tile([P, PACK, H], F32, name=f"w1_raw{g}", align_bytes=64) for g in range(PASSES)]
         w1_rows = w1.rearrange("(g p j) c -> g p j c", p=P, j=PACK)
@@ -74,7 +77,7 @@ def tile_picked_zrandla_relu_po_kernel(
         nc.sync.dma_start(offs_t[:], offs)
         for q in QUADRANT_ORDER:
             nc.sync.dma_start(
-                out=x_scale_window[QUADRANT * q : QUADRANT * q + 4 * PASSES, :].bitcast(I32),
+                out=x_scale_window[QUADRANT * q + 4 : QUADRANT * q + 4 + 4 * PASSES, :].bitcast(I32),
                 in_=x_scales[:, 4 * q : 4 * q + 4, :].bitcast(I32),
             )
 
@@ -94,8 +97,6 @@ def tile_picked_zrandla_relu_po_kernel(
         load_head_scales(FEATURES, w3_scales)
         nc.sync.dma_start(pos1_t[:], pos1)
         nc.sync.dma_start(pos2_t[:], pos2)
-        identity = keep.tile([P, P], F32)
-        make_identity(nc, identity[:])
 
         def deal_words(w, dealt):
             nc.vector.tensor_copy(
@@ -163,7 +164,7 @@ def tile_picked_zrandla_relu_po_kernel(
                 lhsT=w1_codes[g][:, t * P : (t + 1) * P].bitcast(FP8X4),
                 lhsT_scale=w1_scales[g][:, t * P : (t + 1) * P],
                 rhs=x_picked[g][:, batch_cols(b)].bitcast(FP8X4),
-                rhs_scale=x_scales_picked[4 * g : P, batch_cols(b)],
+                rhs_scale=x_scales_picked[4 + 4 * g : P, batch_cols(b)],
                 start=(g == 0 and t == first_pass_tiles[0]),
                 stop=(g == PASSES - 1 and t == PACK - 1),
             )
@@ -252,8 +253,9 @@ def tile_picked_zrandla_relu_po_kernel(
         weight1 = [scratch("weight1_", t) for t in range(PACK)]
         first_score = [scratch("first_score", t) for t in range(PACK)]
         gap = [scratch("gap", 0)[:], scratch("gap", 1)[:], weight0[1], scratch("gap", 3)[:]]
-        term0 = [scratch("term0_", t) for t in range(PACK)]
-        term1 = [scratch("term1_", t) for t in range(PACK)]
+        last_terms = [keep.tile([P, 2, V], F32, name=f"last_terms{d}") for d in range(2)]
+        term0 = [scratch("term0_", t) for t in range(2)] + [last_terms[0][:, t, :] for t in range(2)]
+        term1 = [scratch("term1_", t) for t in range(2)] + [last_terms[1][:, t, :] for t in range(2)]
         centres = slice(0, V)
         centre_halves = (slice(0, V // 2), slice(V // 2, V))
 
@@ -276,15 +278,17 @@ def tile_picked_zrandla_relu_po_kernel(
             nc.scalar.activation(out=weight1[t][:], in_=gap[t], func=ACT.Sigmoid)
 
         def weigh0(t):
-            nc.vector.tensor_tensor(term0[t][:], feature[t][:].indirect(pos1_t[:]), weight0[t], ALU.mult)
+            nc.vector.tensor_tensor(term0[t][:, centres], feature[t][:].indirect(pos1_t[:]), weight0[t], ALU.mult)
 
         def weigh1(t, part):
             nc.vector.tensor_tensor(
                 term1[t][:, part], feature[t][:].indirect(entries(pos2_t, part)), weight1[t][:, part], ALU.mult
             )
 
-        def add_terms(t, part):
-            nc.vector.tensor_tensor(pooled[:, t, part], term0[t][:, part], term1[t][:, part], ALU.add)
+        def add_last_terms(part):
+            nc.vector.tensor_tensor(
+                pooled[:, high_tiles, part], last_terms[0][:, :, part], last_terms[1][:, :, part], ALU.add
+            )
 
         turned = [keep.tile([P, 2, P], F32, name=f"turned{t}") for t in range(SUMMED_ON_TENSOR)]
 
@@ -354,13 +358,11 @@ def tile_picked_zrandla_relu_po_kernel(
 
         for part in centre_halves:
             round_pair(low_tiles, part, nc.scalar.copy)
-        weigh1(3, centre_halves[0])
-        add_terms(2, centres)
-        store(2)
-        weigh1(3, centre_halves[1])
         for part in centre_halves:
-            add_terms(3, part)
-        store(3)
+            weigh1(3, part)
+        for part in centre_halves:
+            add_last_terms(part)
+        store(high_tiles)
         for part in centre_halves:
             round_pair(high_tiles, part, nc.vector.tensor_copy)
         for part in centre_halves:

@@ -51,7 +51,7 @@ def tile_picked_zrandla_relu_po_kernel(
             reused.tile([P, 2 * N], U8, name="score_words_raw", align_bytes=64, offset=SCORE_WORDS_RAW_AT),
             keep.tile([P, 2 * N], U8, name="feature_words_raw", align_bytes=64),
         ]
-        x_scale_window = keep.tile([P, T], U8, align_bytes=64)
+        x_scale_window = keep.tile([P, T], U8, align_bytes=256)
         nc.vector.memset(x_scale_window[:].bitcast(I32), 0)
         warm = keep.tile([P, 2], F32)
         nc.vector.memset(warm[:, 0:1], 0.0)
@@ -63,9 +63,9 @@ def tile_picked_zrandla_relu_po_kernel(
         nc.vector.memset(identity[:], 0.0)
         make_identity(nc, identity[:], nomemset=True)
 
-        w1_raw = [keep.tile([P, PACK, H], F32, name=f"w1_raw{g}", align_bytes=64) for g in range(PASSES)]
+        w1_raw = [keep.tile([P, PACK, H], F32, name=f"w1_raw{g}", align_bytes=256) for g in range(PASSES)]
         w1_rows = w1.rearrange("(g p j) c -> g p j c", p=P, j=PACK)
-        x_window = [keep.tile([P, T], I32, name=f"x_window{g}", align_bytes=64) for g in range(PASSES)]
+        x_window = [keep.tile([P, T], I32, name=f"x_window{g}", align_bytes=256) for g in range(PASSES)]
         offs_t = lists.tile([P, S // ENTRIES_PER_COLUMN], U16)
         pos1_t = lists.tile([P, V // ENTRIES_PER_COLUMN], U16)
         pos2_t = lists.tile([P, V // ENTRIES_PER_COLUMN], U16)
@@ -247,15 +247,14 @@ def tile_picked_zrandla_relu_po_kernel(
         def scratch(name, t):
             return keep.tile([P, V], F32, name=f"{name}{t}")
 
-        pooled = keep.tile([P, PACK, V], F32)
+        pooled = keep.tile([P, PACK, V], F32, align_bytes=256)
         out_rows = out_0.rearrange("(p t) v -> p t v", t=PACK)
         weight0 = [scratch("weight0_", t)[:] for t in range(PACK - 1)] + [pooled[:, PACK - 2, :]]
         weight1 = [scratch("weight1_", t) for t in range(PACK)]
         first_score = [scratch("first_score", t) for t in range(PACK)]
         gap = [scratch("gap", 0)[:], scratch("gap", 1)[:], weight0[1], scratch("gap", 3)[:]]
-        last_terms = [keep.tile([P, 2, V], F32, name=f"last_terms{d}") for d in range(2)]
-        term0 = [scratch("term0_", t) for t in range(2)] + [last_terms[0][:, t, :] for t in range(2)]
-        term1 = [scratch("term1_", t) for t in range(2)] + [last_terms[1][:, t, :] for t in range(2)]
+        term0 = [scratch("term0_", t) for t in range(PACK)]
+        term1 = [scratch("term1_", t) for t in range(PACK)]
         centres = slice(0, V)
         centre_halves = (slice(0, V // 2), slice(V // 2, V))
 
@@ -278,17 +277,15 @@ def tile_picked_zrandla_relu_po_kernel(
             nc.scalar.activation(out=weight1[t][:], in_=gap[t], func=ACT.Sigmoid)
 
         def weigh0(t):
-            nc.vector.tensor_tensor(term0[t][:, centres], feature[t][:].indirect(pos1_t[:]), weight0[t], ALU.mult)
+            nc.vector.tensor_tensor(term0[t][:], feature[t][:].indirect(pos1_t[:]), weight0[t], ALU.mult)
 
         def weigh1(t, part):
             nc.vector.tensor_tensor(
                 term1[t][:, part], feature[t][:].indirect(entries(pos2_t, part)), weight1[t][:, part], ALU.mult
             )
 
-        def add_last_terms(part):
-            nc.vector.tensor_tensor(
-                pooled[:, high_tiles, part], last_terms[0][:, :, part], last_terms[1][:, :, part], ALU.add
-            )
+        def add_terms(t, part):
+            nc.vector.tensor_tensor(pooled[:, t, part], term0[t][:, part], term1[t][:, part], ALU.add)
 
         turned = [keep.tile([P, 2, P], F32, name=f"turned{t}") for t in range(SUMMED_ON_TENSOR)]
 
@@ -350,19 +347,21 @@ def tile_picked_zrandla_relu_po_kernel(
         store(1)
 
         out_grouped = keep.tile([P, V, PACK], BF16, align_bytes=64)
-        out_codes = keep.tile([P, V], U32, align_bytes=64)
-        out_scales = keep.tile([P, V], U8, align_bytes=64)
+        out_codes = keep.tile([P, V], U32, align_bytes=256)
+        out_scales = keep.tile([P, V], U8, align_bytes=256)
 
         def round_pair(tiles, part, copy):
             copy(out=out_grouped[:, part, tiles], in_=pooled[:, tiles, part].rearrange("p t v -> p v t"))
 
         for part in centre_halves:
             round_pair(low_tiles, part, nc.scalar.copy)
+        weigh1(3, centre_halves[0])
+        add_terms(2, centres)
+        store(2)
+        weigh1(3, centre_halves[1])
         for part in centre_halves:
-            weigh1(3, part)
-        for part in centre_halves:
-            add_last_terms(part)
-        store(high_tiles)
+            add_terms(3, part)
+        store(3)
         for part in centre_halves:
             round_pair(high_tiles, part, nc.vector.tensor_copy)
         for part in centre_halves:

@@ -1,7 +1,6 @@
 from contextlib import ExitStack
 
 import concourse.mybir as mybir
-from concourse.masks import make_identity
 
 K, T, S, V, H, N = 1024, 1024, 512, 256, 512, 512
 FLOPS = 2 * S * (K * H + 2 * H * N)
@@ -26,7 +25,6 @@ QUADRANT = 32
 ENTRIES_PER_COLUMN = 16
 QUADRANT_ORDER = (0, 2, 1, 3)
 SCORES, FEATURES = 0, 1
-SUMMED_ON_TENSOR = 2
 
 H_SCALES_AT = 0
 SCORE_WORDS_RAW_AT = 256
@@ -44,8 +42,7 @@ def tile_picked_zrandla_relu_po_kernel(
         lists = ctx.enter_context(tc.tile_pool(name="lists", bufs=1))
         keep = ctx.enter_context(tc.tile_pool(name="keep", bufs=1))
         reused = ctx.enter_context(tc.tile_pool(name="reused", bufs=1))
-        hidden_psum = ctx.enter_context(tc.psum_pool(name="hidden_psum", bufs=1))
-        head_psum = ctx.enter_context(tc.psum_pool(name="head_psum", bufs=4))
+        psum = ctx.enter_context(tc.psum_pool(name="psum", bufs=1))
 
         head_words_raw = [
             reused.tile([P, 2 * N], U8, name="score_words_raw", align_bytes=64, offset=SCORE_WORDS_RAW_AT),
@@ -59,9 +56,6 @@ def tile_picked_zrandla_relu_po_kernel(
         head_scales_raw = [keep.tile([P, N], U8, name=f"head_scales_raw{w}", align_bytes=64) for w in range(2)]
         nc.vector.memset(head_scales_raw[SCORES][:].bitcast(I32), 0)
         nc.vector.memset(head_scales_raw[FEATURES][:].bitcast(I32), 0)
-        identity = keep.tile([P, P], F32)
-        nc.vector.memset(identity[:], 0.0)
-        make_identity(nc, identity[:], nomemset=True)
 
         w1_raw = [keep.tile([P, PACK, H], F32, name=f"w1_raw{g}", align_bytes=256) for g in range(PASSES)]
         w1_rows = w1.rearrange("(g p j) c -> g p j c", p=P, j=PACK)
@@ -142,7 +136,7 @@ def tile_picked_zrandla_relu_po_kernel(
         round_w1(0, high_tiles, tile_whole, nc.vector.tensor_copy)
         round_w1(1, high_tiles, tile_whole, nc.scalar.copy)
 
-        hidden = [hidden_psum.tile([P, PACK, BATCH], F32, name=f"hidden{b}") for b in range(BATCHES)]
+        hidden = [psum.tile([P, PACK, BATCH], F32, name=f"bank{b}") for b in range(BATCHES)]
 
         def entries(list_tile, part):
             return list_tile[:, part.start // ENTRIES_PER_COLUMN : part.stop // ENTRIES_PER_COLUMN]
@@ -220,8 +214,8 @@ def tile_picked_zrandla_relu_po_kernel(
         for part in batch_halves:
             quantize_h(2, part)
 
-        def head_columns(rows, words, scales, t, cols):
-            acc = head_psum.tile([P, S], F32, name="acc")
+        def head_columns(rows, words, scales, t, cols, bank, copy):
+            acc = psum.tile([P, S], F32, name=f"bank{bank}")
             nc.tensor.matmul_mx(
                 out=acc[:, cols],
                 lhsT=words[:, t * 2 * P : (t + 1) * 2 * P].bitcast(FP4X4),
@@ -231,120 +225,62 @@ def tile_picked_zrandla_relu_po_kernel(
                 start=True,
                 stop=True,
             )
-            nc.scalar.copy(out=rows[:, cols], in_=acc[:, cols])
+            copy(out=rows[:, cols], in_=acc[:, cols])
 
         score = [keep.tile([P, S], F32, name=f"score{t}") for t in range(PACK)]
         feature = [keep.tile([P, S], F32, name=f"feature{t}") for t in range(PACK)]
         feature_words = reused.tile([P, 2 * N], U8, align_bytes=64, offset=FEATURE_WORDS_AT)
         feature_scales = reused.tile([P, N], U8, align_bytes=64, offset=FEATURE_SCALES_AT)
 
-        def make_score(t):
-            head_columns(score[t], score_words, score_scales, t, slice(0, S))
+        def make_score(t, bank, copy):
+            head_columns(score[t], score_words, score_scales, t, slice(0, S), bank, copy)
 
-        def make_feature(t):
-            head_columns(feature[t], feature_words, feature_scales, t, slice(0, S))
+        def make_feature(t, bank, copy):
+            head_columns(feature[t], feature_words, feature_scales, t, slice(0, S), bank, copy)
 
-        def scratch(name, t):
-            return keep.tile([P, V], F32, name=f"{name}{t}")
+        def scratch(name):
+            return [keep.tile([P, V], F32, name=f"{name}{t}") for t in range(PACK)]
 
         pooled = keep.tile([P, PACK, V], F32, align_bytes=256)
         out_rows = out_0.rearrange("(p t) v -> p t v", t=PACK)
-        weight0 = [scratch("weight0_", t)[:] for t in range(PACK - 1)] + [pooled[:, PACK - 2, :]]
-        weight1 = [scratch("weight1_", t) for t in range(PACK)]
-        first_score = [scratch("first_score", t) for t in range(PACK)]
-        gap = [scratch("gap", 0)[:], scratch("gap", 1)[:], weight0[1], scratch("gap", 3)[:]]
-        term0 = [scratch("term0_", t) for t in range(PACK)]
-        term1 = [scratch("term1_", t) for t in range(PACK)]
+        first_score, gap, weight = scratch("first_score"), scratch("gap"), scratch("weight")
+        base, rise, term = scratch("base"), scratch("rise"), scratch("term")
         centres = slice(0, V)
         centre_halves = (slice(0, V // 2), slice(V // 2, V))
 
-        def fetch_first(t, part):
-            nc.vector.tensor_copy(first_score[t][:, part], score[t][:].indirect(entries(pos1_t, part)))
+        def scalar_fetch(out, in_):
+            nc.scalar.activation(out=out, in_=in_, func=ACT.Copy)
+
+        def vector_fetch(out, in_):
+            nc.vector.tensor_copy(out, in_)
+
+        def fetch_first(t, part, fetch):
+            fetch(first_score[t][:, part], score[t][:].indirect(entries(pos1_t, part)))
 
         def score_gap(t, part):
             nc.vector.tensor_tensor(
                 gap[t][:, part], score[t][:].indirect(entries(pos2_t, part)), first_score[t][:, part], ALU.subtract
             )
 
-        def gap_by_halves(t):
-            for part in centre_halves:
-                fetch_first(t, part)
-            for part in centre_halves:
-                score_gap(t, part)
+        def make_weight(t):
+            nc.scalar.activation(out=weight[t][:], in_=gap[t][:], func=ACT.Sigmoid, scale=-1.0)
 
-        def make_weights(t):
-            nc.scalar.activation(out=weight0[t], in_=gap[t], func=ACT.Sigmoid, scale=-1.0)
-            nc.scalar.activation(out=weight1[t][:], in_=gap[t], func=ACT.Sigmoid)
+        def fetch_base(t, fetch):
+            fetch(base[t][:], feature[t][:].indirect(pos2_t[:]))
 
-        def weigh0(t):
-            nc.vector.tensor_tensor(term0[t][:], feature[t][:].indirect(pos1_t[:]), weight0[t], ALU.mult)
-
-        def weigh1(t, part):
+        def feature_rise(t, part):
             nc.vector.tensor_tensor(
-                term1[t][:, part], feature[t][:].indirect(entries(pos2_t, part)), weight1[t][:, part], ALU.mult
+                rise[t][:, part], feature[t][:].indirect(entries(pos1_t, part)), base[t][:, part], ALU.subtract
             )
 
-        def add_terms(t, part):
-            nc.vector.tensor_tensor(pooled[:, t, part], term0[t][:, part], term1[t][:, part], ALU.add)
+        def weigh(t, part):
+            nc.vector.tensor_tensor(term[t][:, part], rise[t][:, part], weight[t][:, part], ALU.mult)
 
-        turned = [keep.tile([P, 2, P], F32, name=f"turned{t}") for t in range(SUMMED_ON_TENSOR)]
-
-        def turn_sum(t):
-            turned_psum = hidden_psum.tile([P, 2, P], F32, name=f"hidden{2 * t}")
-            for d, term in enumerate((term0[t], term1[t])):
-                for u in range(2):
-                    nc.tensor.matmul(
-                        turned_psum[:, u, :],
-                        lhsT=term[:, u * P : (u + 1) * P],
-                        rhs=identity[:],
-                        is_transpose=True,
-                        start=(d == 0 and u == 0),
-                        stop=(d == 1 and u == 1),
-                    )
-            nc.scalar.copy(out=turned[t][:], in_=turned_psum[:])
-
-        def turn_back(t):
-            back_psum = hidden_psum.tile([P, 2, P], F32, name=f"hidden{2 * t + 1}")
-            for u in range(2):
-                nc.tensor.transpose(back_psum[:, u, :], turned[t][:, u, :], identity[:])
-            nc.scalar.copy(out=pooled[:, t, :], in_=back_psum[:].rearrange("p u v -> p (u v)"))
+        def add_base(t, part):
+            nc.vector.tensor_tensor(pooled[:, t, part], term[t][:, part], base[t][:, part], ALU.add)
 
         def store(t):
             nc.sync.dma_start(out=out_rows[:, t, :], in_=pooled[:, t, :])
-
-        for b in (0, 1, 3, 2):
-            head_columns(score[0], score_words, score_scales, 0, batch_cols(b))
-        make_score(1)
-        deal_words(FEATURES, feature_words)
-        deal_scales(FEATURES, feature_scales)
-        gap_by_halves(0)
-        gap_by_halves(1)
-        make_feature(0)
-        make_weights(0)
-        weigh0(0)
-        weigh1(0, centres)
-        make_score(2)
-        fetch_first(2, centres)
-        make_feature(1)
-        make_weights(1)
-        weigh0(1)
-        weigh1(1, centres)
-        score_gap(2, centres)
-        make_score(3)
-        gap_by_halves(3)
-        make_feature(2)
-        turn_sum(0)
-        make_feature(3)
-        make_weights(2)
-        weigh0(2)
-        weigh1(2, centres)
-        turn_back(0)
-        store(0)
-        turn_sum(1)
-        make_weights(3)
-        weigh0(3)
-        turn_back(1)
-        store(1)
 
         out_grouped = keep.tile([P, V, PACK], BF16, align_bytes=64)
         out_codes = keep.tile([P, V], U32, align_bytes=256)
@@ -353,15 +289,55 @@ def tile_picked_zrandla_relu_po_kernel(
         def round_pair(tiles, part, copy):
             copy(out=out_grouped[:, part, tiles], in_=pooled[:, tiles, part].rearrange("p t v -> p v t"))
 
+        for b in (0, 1, 3, 2):
+            head_columns(score[0], score_words, score_scales, 0, batch_cols(b), BATCHES + b, nc.scalar.copy)
+        make_score(1, 0, nc.scalar.copy)
+        deal_words(FEATURES, feature_words)
+        deal_scales(FEATURES, feature_scales)
         for part in centre_halves:
-            round_pair(low_tiles, part, nc.scalar.copy)
-        weigh1(3, centre_halves[0])
-        add_terms(2, centres)
+            fetch_first(0, part, vector_fetch)
+        for part in centre_halves:
+            score_gap(0, part)
+        make_feature(0, 1, nc.scalar.copy)
+        fetch_base(0, vector_fetch)
+        fetch_first(1, centres, scalar_fetch)
+        score_gap(1, centres)
+        make_weight(0)
+        feature_rise(0, centres)
+        make_feature(1, 3, nc.scalar.copy)
+        make_feature(2, 4, nc.vector.tensor_copy)
+        weigh(0, centres)
+        fetch_base(1, scalar_fetch)
+        feature_rise(1, centres)
+        make_weight(1)
+        add_base(0, centres)
+        store(0)
+        make_score(2, 2, nc.scalar.copy)
+        weigh(1, centres)
+        fetch_first(2, centres, scalar_fetch)
+        score_gap(2, centres)
+        add_base(1, centres)
+        store(1)
+        fetch_base(2, scalar_fetch)
+        feature_rise(2, centres)
+        make_score(3, 5, nc.scalar.copy)
+        fetch_first(3, centres, scalar_fetch)
+        score_gap(3, centres)
+        make_weight(2)
+        weigh(2, centres)
+        make_feature(3, 6, nc.scalar.copy)
+        fetch_base(3, scalar_fetch)
+        add_base(2, centres)
         store(2)
-        weigh1(3, centre_halves[1])
+        make_weight(3)
+        feature_rise(3, centres)
+        round_pair(low_tiles, centres, nc.scalar.copy)
         for part in centre_halves:
-            add_terms(3, part)
+            weigh(3, part)
+        for part in centre_halves:
+            add_base(3, part)
         store(3)
+
         for part in centre_halves:
             round_pair(high_tiles, part, nc.vector.tensor_copy)
         for part in centre_halves:

@@ -27,11 +27,10 @@ QUADRANT_ORDER = (0, 2, 1, 3)
 SCORES, FEATURES = 0, 1
 
 H_SCALES_AT = 0
-SCORE_WORDS_RAW_AT = 256
+FEATURE_SCALES_RAW_AT = 256
 VECTOR_BATCH_AT = 512
-LAST_BATCH_AT = 2048
-FEATURE_SCALES_AT = LAST_BATCH_AT
-FEATURE_WORDS_AT = LAST_BATCH_AT + N
+SCALAR_BATCHES_AT = 2048
+LAST_GAP_AT = 6144
 
 
 def tile_picked_zrandla_relu_po_kernel(
@@ -45,15 +44,18 @@ def tile_picked_zrandla_relu_po_kernel(
         psum = ctx.enter_context(tc.psum_pool(name="psum", bufs=1))
 
         head_words_raw = [
-            reused.tile([P, 2 * N], U8, name="score_words_raw", align_bytes=64, offset=SCORE_WORDS_RAW_AT),
-            keep.tile([P, 2 * N], U8, name="feature_words_raw", align_bytes=64),
+            keep.tile([P, 2 * N], U8, name="score_words_raw", align_bytes=64),
+            reused.tile([P, 2 * N], U8, name="feature_words_raw", align_bytes=64, offset=SCALAR_BATCHES_AT),
         ]
         x_scale_window = keep.tile([P, T], U8, align_bytes=256)
         nc.vector.memset(x_scale_window[:].bitcast(I32), 0)
         warm = keep.tile([P, 2], F32)
         nc.vector.memset(warm[:, 0:1], 0.0)
         nc.scalar.activation(out=warm[:, 1:2], in_=warm[:, 0:1], func=ACT.Sigmoid)
-        head_scales_raw = [keep.tile([P, N], U8, name=f"head_scales_raw{w}", align_bytes=64) for w in range(2)]
+        head_scales_raw = [
+            keep.tile([P, N], U8, name="score_scales_raw", align_bytes=64),
+            reused.tile([P, N], U8, name="feature_scales_raw", align_bytes=64, offset=FEATURE_SCALES_RAW_AT),
+        ]
         nc.vector.memset(head_scales_raw[SCORES][:].bitcast(I32), 0)
         nc.vector.memset(head_scales_raw[FEATURES][:].bitcast(I32), 0)
 
@@ -93,7 +95,7 @@ def tile_picked_zrandla_relu_po_kernel(
         nc.sync.dma_start(pos2_t[:], pos2)
 
         def deal_words(w, dealt):
-            nc.vector.tensor_copy(
+            nc.scalar.copy(
                 out=dealt[:].bitcast(U16).rearrange("p (t c) -> p t c", t=PACK),
                 in_=head_words_raw[w][:].bitcast(U16).rearrange("p (c t) -> p t c", t=PACK),
             )
@@ -180,12 +182,15 @@ def tile_picked_zrandla_relu_po_kernel(
         for b in range(1, BATCHES):
             pick_words(1, batch_cols(b))
         score_words = keep.tile([P, 2 * N], U8, align_bytes=64)
+        feature_words = keep.tile([P, 2 * N], U8, align_bytes=64)
+        feature_scales = keep.tile([P, N], U8, align_bytes=64)
         deal_words(SCORES, score_words)
+        deal_words(FEATURES, feature_words)
+        deal_scales(FEATURES, feature_scales)
 
-        h_grouped = [keep.tile([P, BATCH, PACK], BF16, name=f"h_grouped{b}", align_bytes=64) for b in range(2)] + [
-            reused.tile([P, BATCH, PACK], BF16, name="h_grouped2", align_bytes=64, offset=LAST_BATCH_AT),
-            reused.tile([P, BATCH, PACK], BF16, name="h_grouped3", align_bytes=64, offset=VECTOR_BATCH_AT),
-        ]
+        scalar_batches = reused.tile([P, BATCHES - 1, BATCH, PACK], BF16, align_bytes=64, offset=SCALAR_BATCHES_AT)
+        vector_batch = reused.tile([P, BATCH, PACK], BF16, align_bytes=64, offset=VECTOR_BATCH_AT)
+        h_grouped = [scalar_batches[:, b] for b in range(BATCHES - 1)] + [vector_batch[:]]
         batch_whole = slice(0, BATCH)
         batch_halves = (slice(0, BATCH // 2), slice(BATCH // 2, BATCH))
 
@@ -203,12 +208,12 @@ def tile_picked_zrandla_relu_po_kernel(
             )
 
         for b in range(2):
-            nc.scalar.activation(out=h_grouped[b][:], in_=close_batch(b), func=ACT.Relu)
+            nc.scalar.activation(out=h_grouped[b], in_=close_batch(b), func=ACT.Relu)
         last_sums = close_batch(2)
         for part in batch_halves:
             nc.scalar.activation(out=h_grouped[2][:, part, :], in_=last_sums[:, part, :], func=ACT.Relu)
         quantize_h(0, batch_whole)
-        nc.vector.tensor_scalar_max(h_grouped[3][:], close_batch(3), 0.0)
+        nc.vector.tensor_scalar_max(h_grouped[3], close_batch(3), 0.0)
         quantize_h(1, batch_whole)
         quantize_h(3, batch_whole)
         for part in batch_halves:
@@ -227,23 +232,25 @@ def tile_picked_zrandla_relu_po_kernel(
             )
             copy(out=rows[:, cols], in_=acc[:, cols])
 
-        score = [keep.tile([P, S], F32, name=f"score{t}") for t in range(PACK)]
+        score = [keep.tile([P, S], F32, name="score1" if t == 2 else f"score{t}") for t in range(PACK)]
         feature = [keep.tile([P, S], F32, name=f"feature{t}") for t in range(PACK)]
-        feature_words = reused.tile([P, 2 * N], U8, align_bytes=64, offset=FEATURE_WORDS_AT)
-        feature_scales = reused.tile([P, N], U8, align_bytes=64, offset=FEATURE_SCALES_AT)
 
-        def make_score(t, bank, copy):
-            head_columns(score[t], score_words, score_scales, t, slice(0, S), bank, copy)
+        points, early_points, late_points = slice(0, S), slice(0, S // 2), slice(S // 2, S)
 
-        def make_feature(t, bank, copy):
-            head_columns(feature[t], feature_words, feature_scales, t, slice(0, S), bank, copy)
+        def make_score(t, cols, bank, copy):
+            head_columns(score[t], score_words, score_scales, t, cols, bank, copy)
+
+        def make_feature(t, cols, bank, copy):
+            head_columns(feature[t], feature_words, feature_scales, t, cols, bank, copy)
 
         def scratch(name):
             return [keep.tile([P, V], F32, name=f"{name}{t}") for t in range(PACK)]
 
         pooled = keep.tile([P, PACK, V], F32, align_bytes=256)
         out_rows = out_0.rearrange("(p t) v -> p t v", t=PACK)
-        first_score, gap, weight = scratch("first_score"), scratch("gap"), scratch("weight")
+        first_score, weight = scratch("first_score"), scratch("weight")
+        gap = [keep.tile([P, V], F32, name=f"gap{t}") for t in range(PACK - 1)]
+        gap.append(reused.tile([P, V], F32, name="last_gap", align_bytes=64, offset=LAST_GAP_AT))
         base, rise, term = scratch("base"), scratch("rise"), scratch("term")
         centres = slice(0, V)
         centre_halves = (slice(0, V // 2), slice(V // 2, V))
@@ -265,8 +272,8 @@ def tile_picked_zrandla_relu_po_kernel(
         def make_weight(t):
             nc.scalar.activation(out=weight[t][:], in_=gap[t][:], func=ACT.Sigmoid, scale=-1.0)
 
-        def fetch_base(t, fetch):
-            fetch(base[t][:], feature[t][:].indirect(pos2_t[:]))
+        def fetch_base(t, part, fetch):
+            fetch(base[t][:, part], feature[t][:].indirect(entries(pos2_t, part)))
 
         def feature_rise(t, part):
             nc.vector.tensor_tensor(
@@ -282,55 +289,58 @@ def tile_picked_zrandla_relu_po_kernel(
         def store(t):
             nc.sync.dma_start(out=out_rows[:, t, :], in_=pooled[:, t, :])
 
-        out_grouped = keep.tile([P, V, PACK], BF16, align_bytes=64)
+        out_grouped = reused.tile([P, V, PACK], BF16, align_bytes=64, offset=LAST_GAP_AT)
         out_codes = keep.tile([P, V], U32, align_bytes=256)
         out_scales = keep.tile([P, V], U8, align_bytes=256)
 
         def round_pair(tiles, part, copy):
             copy(out=out_grouped[:, part, tiles], in_=pooled[:, tiles, part].rearrange("p t v -> p v t"))
 
-        for b in (0, 1, 3, 2):
-            head_columns(score[0], score_words, score_scales, 0, batch_cols(b), BATCHES + b, nc.scalar.copy)
-        make_score(1, 0, nc.scalar.copy)
-        deal_words(FEATURES, feature_words)
-        deal_scales(FEATURES, feature_scales)
+        on_scalar, on_vector = nc.scalar.copy, nc.vector.tensor_copy
+        make_score(0, early_points, 4, on_scalar)
+        make_score(0, batch_cols(3), 0, on_scalar)
+        make_score(0, batch_cols(2), 1, on_scalar)
+        make_score(1, early_points, 5, on_vector)
+        make_feature(0, early_points, 6, on_vector)
+        make_feature(1, early_points, 7, on_vector)
         for part in centre_halves:
             fetch_first(0, part, vector_fetch)
         for part in centre_halves:
             score_gap(0, part)
-        make_feature(0, 1, nc.scalar.copy)
-        fetch_base(0, vector_fetch)
+        make_score(1, late_points, 3, on_scalar)
+        make_feature(0, late_points, 2, on_scalar)
+        make_feature(1, late_points, 4, on_vector)
         fetch_first(1, centres, scalar_fetch)
         score_gap(1, centres)
-        make_weight(0)
+        fetch_base(0, centres, scalar_fetch)
         feature_rise(0, centres)
-        make_feature(1, 3, nc.scalar.copy)
-        make_feature(2, 4, nc.vector.tensor_copy)
+        make_score(2, points, 0, on_vector)
+        make_weight(0)
         weigh(0, centres)
-        fetch_base(1, scalar_fetch)
+        fetch_base(1, centres, scalar_fetch)
         feature_rise(1, centres)
-        make_weight(1)
         add_base(0, centres)
         store(0)
-        make_score(2, 2, nc.scalar.copy)
-        weigh(1, centres)
+        make_feature(2, points, 1, on_scalar)
+        make_weight(1)
         fetch_first(2, centres, scalar_fetch)
         score_gap(2, centres)
+        weigh(1, centres)
+        fetch_base(2, centres, scalar_fetch)
+        feature_rise(2, centres)
         add_base(1, centres)
         store(1)
-        fetch_base(2, scalar_fetch)
-        feature_rise(2, centres)
-        make_score(3, 5, nc.scalar.copy)
+        make_score(3, points, 5, on_scalar)
+        make_feature(3, points, 6, on_scalar)
         fetch_first(3, centres, scalar_fetch)
         score_gap(3, centres)
         make_weight(2)
         weigh(2, centres)
-        make_feature(3, 6, nc.scalar.copy)
-        fetch_base(3, scalar_fetch)
+        fetch_base(3, centres, scalar_fetch)
+        feature_rise(3, centres)
         add_base(2, centres)
         store(2)
         make_weight(3)
-        feature_rise(3, centres)
         round_pair(low_tiles, centres, nc.scalar.copy)
         for part in centre_halves:
             weigh(3, part)

@@ -30,7 +30,8 @@ H_SCALES_AT = 0
 FEATURE_SCALES_RAW_AT = 256
 VECTOR_BATCH_AT = 512
 SCALAR_BATCHES_AT = 2048
-LAST_GAP_AT = 6144
+SECOND_PASS_AT = 6656
+EARLY_TILES_AT = (512, 2560, 4608)
 
 
 def tile_picked_zrandla_relu_po_kernel(
@@ -94,8 +95,8 @@ def tile_picked_zrandla_relu_po_kernel(
         nc.sync.dma_start(pos1_t[:], pos1)
         nc.sync.dma_start(pos2_t[:], pos2)
 
-        def deal_words(w, dealt):
-            nc.scalar.copy(
+        def deal_words(w, dealt, copy):
+            copy(
                 out=dealt[:].bitcast(U16).rearrange("p (t c) -> p t c", t=PACK),
                 in_=head_words_raw[w][:].bitcast(U16).rearrange("p (c t) -> p t c", t=PACK),
             )
@@ -111,7 +112,10 @@ def tile_picked_zrandla_relu_po_kernel(
         x_scales_picked = keep.tile([P, S], U8, align_bytes=64)
         nc.vector.tensor_copy(x_scales_picked[:], x_scale_window[:].indirect(offs_t[:]))
 
-        w1_grouped = [keep.tile([P, PACK, P, PACK], BF16, name=f"w1_grouped{g}", align_bytes=64) for g in range(PASSES)]
+        w1_grouped = [
+            keep.tile([P, PACK, P, PACK], BF16, name="w1_grouped0", align_bytes=64),
+            reused.tile([P, PACK, P, PACK], BF16, name="w1_grouped1", align_bytes=64, offset=SECOND_PASS_AT),
+        ]
         w1_codes = [keep.tile([P, H], U32, name=f"w1_codes{g}", align_bytes=64) for g in range(PASSES)]
         w1_scales = [keep.tile([P, H], U8, name=f"w1_scales{g}", align_bytes=64) for g in range(PASSES)]
 
@@ -183,9 +187,9 @@ def tile_picked_zrandla_relu_po_kernel(
             pick_words(1, batch_cols(b))
         score_words = keep.tile([P, 2 * N], U8, align_bytes=64)
         feature_words = keep.tile([P, 2 * N], U8, align_bytes=64)
-        feature_scales = keep.tile([P, N], U8, align_bytes=64)
-        deal_words(SCORES, score_words)
-        deal_words(FEATURES, feature_words)
+        deal_words(SCORES, score_words, nc.scalar.copy)
+        deal_words(FEATURES, feature_words, nc.scalar.copy)
+        feature_scales = reused.tile([P, N], U8, align_bytes=64, offset=SECOND_PASS_AT)
         deal_scales(FEATURES, feature_scales)
 
         scalar_batches = reused.tile([P, BATCHES - 1, BATCH, PACK], BF16, align_bytes=64, offset=SCALAR_BATCHES_AT)
@@ -232,8 +236,12 @@ def tile_picked_zrandla_relu_po_kernel(
             )
             copy(out=rows[:, cols], in_=acc[:, cols])
 
-        score = [keep.tile([P, S], F32, name="score1" if t == 2 else f"score{t}") for t in range(PACK)]
+        score = [keep.tile([P, S], F32, name=f"score{t}") for t in range(PACK)]
         feature = [keep.tile([P, S], F32, name=f"feature{t}") for t in range(PACK)]
+        score[1], feature[0], feature[1] = [
+            reused.tile([P, S], F32, name=f"early_tile{i}", align_bytes=64, offset=at)
+            for i, at in enumerate(EARLY_TILES_AT)
+        ]
 
         points, early_points, late_points = slice(0, S), slice(0, S // 2), slice(S // 2, S)
 
@@ -249,8 +257,7 @@ def tile_picked_zrandla_relu_po_kernel(
         pooled = keep.tile([P, PACK, V], F32, align_bytes=256)
         out_rows = out_0.rearrange("(p t) v -> p t v", t=PACK)
         first_score, weight = scratch("first_score"), scratch("weight")
-        gap = [keep.tile([P, V], F32, name=f"gap{t}") for t in range(PACK - 1)]
-        gap.append(reused.tile([P, V], F32, name="last_gap", align_bytes=64, offset=LAST_GAP_AT))
+        gap = scratch("gap")
         base, rise, term = scratch("base"), scratch("rise"), scratch("term")
         centres = slice(0, V)
         centre_halves = (slice(0, V // 2), slice(V // 2, V))
@@ -289,7 +296,7 @@ def tile_picked_zrandla_relu_po_kernel(
         def store(t):
             nc.sync.dma_start(out=out_rows[:, t, :], in_=pooled[:, t, :])
 
-        out_grouped = reused.tile([P, V, PACK], BF16, align_bytes=64, offset=LAST_GAP_AT)
+        out_grouped = keep.tile([P, V, PACK], BF16, align_bytes=64)
         out_codes = keep.tile([P, V], U32, align_bytes=256)
         out_scales = keep.tile([P, V], U8, align_bytes=256)
 
@@ -297,47 +304,51 @@ def tile_picked_zrandla_relu_po_kernel(
             copy(out=out_grouped[:, part, tiles], in_=pooled[:, tiles, part].rearrange("p t v -> p v t"))
 
         on_scalar, on_vector = nc.scalar.copy, nc.vector.tensor_copy
-        make_score(0, early_points, 4, on_scalar)
+        make_score(0, batch_cols(0), 4, on_scalar)
+        make_score(0, batch_cols(1), 5, on_scalar)
         make_score(0, batch_cols(3), 0, on_scalar)
-        make_score(0, batch_cols(2), 1, on_scalar)
-        make_score(1, early_points, 5, on_vector)
-        make_feature(0, early_points, 6, on_vector)
-        make_feature(1, early_points, 7, on_vector)
+        make_score(0, batch_cols(2), 4, on_scalar)
+        make_score(1, early_points, 6, on_vector)
+        make_feature(0, early_points, 7, on_vector)
+        make_feature(1, early_points, 1, on_vector)
         for part in centre_halves:
             fetch_first(0, part, vector_fetch)
         for part in centre_halves:
             score_gap(0, part)
         make_score(1, late_points, 3, on_scalar)
         make_feature(0, late_points, 2, on_scalar)
-        make_feature(1, late_points, 4, on_vector)
+        fetch_base(0, centres, vector_fetch)
         fetch_first(1, centres, scalar_fetch)
         score_gap(1, centres)
-        fetch_base(0, centres, scalar_fetch)
         feature_rise(0, centres)
-        make_score(2, points, 0, on_vector)
-        make_weight(0)
-        weigh(0, centres)
+        make_feature(2, early_points, 6, on_vector)
+        make_feature(1, late_points, 5, on_scalar)
+        make_score(2, points, 0, on_scalar)
         fetch_base(1, centres, scalar_fetch)
         feature_rise(1, centres)
-        add_base(0, centres)
-        store(0)
-        make_feature(2, points, 1, on_scalar)
-        make_weight(1)
+        make_weight(0)
+        weigh(0, centres)
         fetch_first(2, centres, scalar_fetch)
         score_gap(2, centres)
+        add_base(0, centres)
+        store(0)
+        make_feature(2, late_points, 7, on_scalar)
+        make_score(3, points, 1, on_scalar)
+        make_weight(1)
         weigh(1, centres)
         fetch_base(2, centres, scalar_fetch)
         feature_rise(2, centres)
         add_base(1, centres)
         store(1)
-        make_score(3, points, 5, on_scalar)
-        make_feature(3, points, 6, on_scalar)
         fetch_first(3, centres, scalar_fetch)
         score_gap(3, centres)
+        make_feature(3, points, 4, on_scalar)
         make_weight(2)
         weigh(2, centres)
-        fetch_base(3, centres, scalar_fetch)
-        feature_rise(3, centres)
+        fetch_base(3, centre_halves[0], scalar_fetch)
+        feature_rise(3, centre_halves[0])
+        fetch_base(3, centre_halves[1], scalar_fetch)
+        feature_rise(3, centre_halves[1])
         add_base(2, centres)
         store(2)
         make_weight(3)

@@ -22,6 +22,8 @@ PASSES = K // (P * PACK)
 BATCH = 128
 BATCHES = S // BATCH
 QUADRANT = 32
+ROWS = 4
+X_SCALES_FROM = 4
 ENTRIES_PER_COLUMN = 16
 QUADRANT_ORDER = (0, 2, 1, 3)
 SCORES, FEATURES = 0, 1
@@ -31,7 +33,7 @@ FEATURE_SCALES_RAW_AT = 256
 VECTOR_BATCH_AT = 512
 SCALAR_BATCHES_AT = 2048
 SECOND_PASS_AT = 6656
-EARLY_TILES_AT = (512, 2560, 4608)
+EARLY_TILES_AT = {("score", 1): 512, ("feature", 0): 2560, ("feature", 1): 4608}
 
 
 def tile_picked_zrandla_relu_po_kernel(
@@ -73,16 +75,17 @@ def tile_picked_zrandla_relu_po_kernel(
         load_x(0)
         nc.sync.dma_start(offs_t[:], offs)
         for q in QUADRANT_ORDER:
+            first_row = QUADRANT * q + X_SCALES_FROM
             nc.sync.dma_start(
-                out=x_scale_window[QUADRANT * q + 4 : QUADRANT * q + 4 + 4 * PASSES, :].bitcast(I32),
-                in_=x_scales[:, 4 * q : 4 * q + 4, :].bitcast(I32),
+                out=x_scale_window[first_row : first_row + ROWS * PASSES, :].bitcast(I32),
+                in_=x_scales[:, ROWS * q : ROWS * q + ROWS, :].bitcast(I32),
             )
 
         def load_head_scales(w, scales):
             for q in QUADRANT_ORDER:
                 nc.sync.dma_start(
-                    out=head_scales_raw[w][QUADRANT * q : QUADRANT * q + 4, :].bitcast(I32),
-                    in_=scales[0, 4 * q : 4 * q + 4, :].bitcast(I32),
+                    out=head_scales_raw[w][QUADRANT * q : QUADRANT * q + ROWS, :].bitcast(I32),
+                    in_=scales[0, ROWS * q : ROWS * q + ROWS, :].bitcast(I32),
                 )
 
         nc.sync.dma_start(out=w1_raw[0][:], in_=w1_rows[0])
@@ -95,8 +98,8 @@ def tile_picked_zrandla_relu_po_kernel(
         nc.sync.dma_start(pos1_t[:], pos1)
         nc.sync.dma_start(pos2_t[:], pos2)
 
-        def deal_words(w, dealt, copy):
-            copy(
+        def deal_words(w, dealt):
+            nc.scalar.copy(
                 out=dealt[:].bitcast(U16).rearrange("p (t c) -> p t c", t=PACK),
                 in_=head_words_raw[w][:].bitcast(U16).rearrange("p (c t) -> p t c", t=PACK),
             )
@@ -164,7 +167,7 @@ def tile_picked_zrandla_relu_po_kernel(
                 lhsT=w1_codes[g][:, t * P : (t + 1) * P].bitcast(FP8X4),
                 lhsT_scale=w1_scales[g][:, t * P : (t + 1) * P],
                 rhs=x_picked[g][:, batch_cols(b)].bitcast(FP8X4),
-                rhs_scale=x_scales_picked[4 + 4 * g : P, batch_cols(b)],
+                rhs_scale=x_scales_picked[X_SCALES_FROM + ROWS * g : P, batch_cols(b)],
                 start=(g == 0 and t == first_pass_tiles[0]),
                 stop=(g == PASSES - 1 and t == PACK - 1),
             )
@@ -187,8 +190,8 @@ def tile_picked_zrandla_relu_po_kernel(
             pick_words(1, batch_cols(b))
         score_words = keep.tile([P, 2 * N], U8, align_bytes=64)
         feature_words = keep.tile([P, 2 * N], U8, align_bytes=64)
-        deal_words(SCORES, score_words, nc.scalar.copy)
-        deal_words(FEATURES, feature_words, nc.scalar.copy)
+        deal_words(SCORES, score_words)
+        deal_words(FEATURES, feature_words)
         feature_scales = reused.tile([P, N], U8, align_bytes=64, offset=SECOND_PASS_AT)
         deal_scales(FEATURES, feature_scales)
 
@@ -236,12 +239,13 @@ def tile_picked_zrandla_relu_po_kernel(
             )
             copy(out=rows[:, cols], in_=acc[:, cols])
 
-        score = [keep.tile([P, S], F32, name=f"score{t}") for t in range(PACK)]
-        feature = [keep.tile([P, S], F32, name=f"feature{t}") for t in range(PACK)]
-        score[1], feature[0], feature[1] = [
-            reused.tile([P, S], F32, name=f"early_tile{i}", align_bytes=64, offset=at)
-            for i, at in enumerate(EARLY_TILES_AT)
-        ]
+        def head_rows(name, t):
+            if (name, t) in EARLY_TILES_AT:
+                return reused.tile([P, S], F32, name=f"{name}{t}", align_bytes=64, offset=EARLY_TILES_AT[name, t])
+            return keep.tile([P, S], F32, name=f"{name}{t}")
+
+        score = [head_rows("score", t) for t in range(PACK)]
+        feature = [head_rows("feature", t) for t in range(PACK)]
 
         points, early_points, late_points = slice(0, S), slice(0, S // 2), slice(S // 2, S)
 
@@ -256,8 +260,7 @@ def tile_picked_zrandla_relu_po_kernel(
 
         pooled = keep.tile([P, PACK, V], F32, align_bytes=256)
         out_rows = out_0.rearrange("(p t) v -> p t v", t=PACK)
-        first_score, weight = scratch("first_score"), scratch("weight")
-        gap = scratch("gap")
+        first_score, weight, gap = scratch("first_score"), scratch("weight"), scratch("gap")
         base, rise, term = scratch("base"), scratch("rise"), scratch("term")
         centres = slice(0, V)
         centre_halves = (slice(0, V // 2), slice(V // 2, V))
@@ -345,10 +348,9 @@ def tile_picked_zrandla_relu_po_kernel(
         make_feature(3, points, 4, on_scalar)
         make_weight(2)
         weigh(2, centres)
-        fetch_base(3, centre_halves[0], scalar_fetch)
-        feature_rise(3, centre_halves[0])
-        fetch_base(3, centre_halves[1], scalar_fetch)
-        feature_rise(3, centre_halves[1])
+        for part in centre_halves:
+            fetch_base(3, part, scalar_fetch)
+            feature_rise(3, part)
         add_base(2, centres)
         store(2)
         make_weight(3)
@@ -368,9 +370,8 @@ def tile_picked_zrandla_relu_po_kernel(
                 in_=out_grouped[:, part, :].rearrange("p v t -> p (v t)"),
             )
         nc.sync.dma_start(out=out_1[0].rearrange("p c r -> p (c r)").bitcast(I32), in_=out_codes[:].bitcast(I32))
-        for q in range(P // QUADRANT):
-            queue = nc.scalar if q % 2 else nc.sync
+        for q, queue in enumerate((nc.sync, nc.sync, nc.sync, nc.scalar)):
             queue.dma_start(
-                out=out_2[0, 4 * q : 4 * q + 4, :].bitcast(I32),
-                in_=out_scales[QUADRANT * q : QUADRANT * q + 4, :].bitcast(I32),
+                out=out_2[0, ROWS * q : ROWS * q + ROWS, :].bitcast(I32),
+                in_=out_scales[QUADRANT * q : QUADRANT * q + ROWS, :].bitcast(I32),
             )

@@ -33,7 +33,8 @@ FEATURE_SCALES_RAW_AT = 256
 VECTOR_BATCH_AT = 512
 SCALAR_BATCHES_AT = 2048
 SECOND_PASS_AT = 6656
-EARLY_TILES_AT = {("score", 1): 512, ("feature", 0): 2560, ("feature", 1): 4608}
+EARLY_TILES_AT = {("score", 1): 512, ("feature", 0): 2560, ("feature", 1): 4608, ("score", 3): 10752}
+FIRST_RISE_AT = 10752
 
 
 def tile_picked_zrandla_relu_po_kernel(
@@ -262,6 +263,7 @@ def tile_picked_zrandla_relu_po_kernel(
         out_rows = out_0.rearrange("(p t) v -> p t v", t=PACK)
         first_score, weight, gap = scratch("first_score"), scratch("weight"), scratch("gap")
         base, rise, term = scratch("base"), scratch("rise"), scratch("term")
+        rise[0] = reused.tile([P, V], F32, name="first_rise", align_bytes=64, offset=FIRST_RISE_AT)
         centres = slice(0, V)
         centre_halves = (slice(0, V // 2), slice(V // 2, V))
 
@@ -314,38 +316,37 @@ def tile_picked_zrandla_relu_po_kernel(
         make_score(1, early_points, 6, on_vector)
         make_feature(0, early_points, 7, on_vector)
         make_feature(1, early_points, 1, on_vector)
+        make_score(1, late_points, 3, on_vector)
+        make_feature(0, late_points, 2, on_scalar)
+        make_feature(1, late_points, 5, on_scalar)
         for part in centre_halves:
             fetch_first(0, part, vector_fetch)
+        fetch_first(1, centres, scalar_fetch)
         for part in centre_halves:
             score_gap(0, part)
-        make_score(1, late_points, 3, on_scalar)
-        make_feature(0, late_points, 2, on_scalar)
-        fetch_base(0, centres, vector_fetch)
-        fetch_first(1, centres, scalar_fetch)
+        fetch_base(0, centres, scalar_fetch)
         score_gap(1, centres)
-        feature_rise(0, centres)
-        make_feature(2, early_points, 6, on_vector)
-        make_feature(1, late_points, 5, on_scalar)
-        make_score(2, points, 0, on_scalar)
         fetch_base(1, centres, scalar_fetch)
-        feature_rise(1, centres)
+        feature_rise(0, centres)
         make_weight(0)
-        weigh(0, centres)
-        fetch_first(2, centres, scalar_fetch)
-        score_gap(2, centres)
-        add_base(0, centres)
-        store(0)
-        make_feature(2, late_points, 7, on_scalar)
-        make_score(3, points, 1, on_scalar)
+        feature_rise(1, centres)
         make_weight(1)
+        weigh(0, centres)
+        make_score(2, points, 0, on_scalar)
         weigh(1, centres)
-        fetch_base(2, centres, scalar_fetch)
-        feature_rise(2, centres)
+        make_score(3, points, 1, on_vector)
+        nc.gpsimd.tensor_tensor(pooled[:, 0, :], term[0][:], base[0][:], ALU.add)
+        store(0)
+        make_feature(2, points, 6, on_scalar)
+        fetch_first(2, centres, scalar_fetch)
         add_base(1, centres)
         store(1)
+        fetch_base(2, centres, scalar_fetch)
+        score_gap(2, centres)
         fetch_first(3, centres, scalar_fetch)
-        score_gap(3, centres)
+        feature_rise(2, centres)
         make_feature(3, points, 4, on_scalar)
+        score_gap(3, centres)
         make_weight(2)
         weigh(2, centres)
         for part in centre_halves:

@@ -316,14 +316,12 @@ def tile_picked_zrandla_relu_po_kernel(
         make_score(1, early_points, 6, on_vector)
         make_feature(0, early_points, 7, on_vector)
         make_feature(1, early_points, 1, on_vector)
-        make_score(1, late_points, 3, on_vector)
+        make_score(1, late_points, 3, on_scalar)
         make_feature(0, late_points, 2, on_scalar)
-        make_feature(1, late_points, 5, on_scalar)
-        for part in centre_halves:
-            fetch_first(0, part, vector_fetch)
+        fetch_first(0, centres, vector_fetch)
+        make_feature(1, late_points, 5, on_vector)
         fetch_first(1, centres, scalar_fetch)
-        for part in centre_halves:
-            score_gap(0, part)
+        score_gap(0, centres)
         fetch_base(0, centres, scalar_fetch)
         score_gap(1, centres)
         fetch_base(1, centres, scalar_fetch)

@@ -33,8 +33,8 @@ FEATURE_SCALES_RAW_AT = 256
 VECTOR_BATCH_AT = 512
 SCALAR_BATCHES_AT = 2048
 SECOND_PASS_AT = 6656
-EARLY_TILES_AT = {("score", 1): 512, ("feature", 0): 2560, ("feature", 1): 4608, ("score", 3): 10752}
-FIRST_RISE_AT = 10752
+EARLY_TILES_AT = {("score", 1): 512, ("feature", 0): 2560, ("feature", 1): 4608, ("score", 3): 10752, ("feature", 3): 12800}
+FIRST_RISE_AT = 12288
 
 
 def tile_picked_zrandla_relu_po_kernel(
@@ -227,17 +227,24 @@ def tile_picked_zrandla_relu_po_kernel(
         for part in batch_halves:
             quantize_h(2, part)
 
+        def product_pieces(cols):
+            if cols.stop - cols.start == 3 * BATCH:
+                cut = cols.start + 2 * BATCH
+                return (slice(cols.start, cut), slice(cut, cols.stop))
+            return (cols,)
+
         def head_columns(rows, words, scales, t, cols, bank, copy):
             acc = psum.tile([P, S], F32, name=f"bank{bank}")
-            nc.tensor.matmul_mx(
-                out=acc[:, cols],
-                lhsT=words[:, t * 2 * P : (t + 1) * 2 * P].bitcast(FP4X4),
-                lhsT_scale=scales[:, t * P : (t + 1) * P],
-                rhs=h_codes[:, cols].bitcast(FP8X4),
-                rhs_scale=h_scales[:, cols],
-                start=True,
-                stop=True,
-            )
+            for piece in product_pieces(cols):
+                nc.tensor.matmul_mx(
+                    out=acc[:, piece],
+                    lhsT=words[:, t * 2 * P : (t + 1) * 2 * P].bitcast(FP4X4),
+                    lhsT_scale=scales[:, t * P : (t + 1) * P],
+                    rhs=h_codes[:, piece].bitcast(FP8X4),
+                    rhs_scale=h_scales[:, piece],
+                    start=True,
+                    stop=True,
+                )
             copy(out=rows[:, cols], in_=acc[:, cols])
 
         def head_rows(name, t):
@@ -333,6 +340,7 @@ def tile_picked_zrandla_relu_po_kernel(
         make_score(2, points, 0, on_scalar)
         weigh(1, centres)
         make_score(3, points, 1, on_vector)
+        make_feature(3, batch_cols(3), 7, on_vector)
         nc.gpsimd.tensor_tensor(pooled[:, 0, :], term[0][:], base[0][:], ALU.add)
         store(0)
         make_feature(2, points, 6, on_scalar)
@@ -343,19 +351,19 @@ def tile_picked_zrandla_relu_po_kernel(
         score_gap(2, centres)
         fetch_first(3, centres, scalar_fetch)
         feature_rise(2, centres)
-        make_feature(3, points, 4, on_scalar)
+        make_feature(3, slice(0, 3 * BATCH), 4, on_scalar)
         score_gap(3, centres)
         make_weight(2)
         weigh(2, centres)
         for part in centre_halves:
             fetch_base(3, part, scalar_fetch)
             feature_rise(3, part)
-        add_base(2, centres)
-        store(2)
         make_weight(3)
         round_pair(low_tiles, centres, nc.scalar.copy)
         for part in centre_halves:
             weigh(3, part)
+            add_base(2, part)
+        store(2)
         for part in centre_halves:
             add_base(3, part)
         store(3)

@@ -33,7 +33,8 @@ FEATURE_SCALES_RAW_AT = 256
 VECTOR_BATCH_AT = 512
 SCALAR_BATCHES_AT = 2048
 SECOND_PASS_AT = 6656
-EARLY_TILES_AT = {("score", 1): 512, ("feature", 0): 2560, ("feature", 1): 4608, ("score", 3): 10752, ("feature", 3): 12800}
+EARLY_TILES_AT = {("score", 1): 512, ("feature", 0): 2560, ("feature", 1): 4608}
+LATE_TILES_AT = {("score", 3): 10752, ("feature", 3): 12800}
 FIRST_RISE_AT = 12288
 
 
@@ -248,8 +249,9 @@ def tile_picked_zrandla_relu_po_kernel(
             copy(out=rows[:, cols], in_=acc[:, cols])
 
         def head_rows(name, t):
-            if (name, t) in EARLY_TILES_AT:
-                return reused.tile([P, S], F32, name=f"{name}{t}", align_bytes=64, offset=EARLY_TILES_AT[name, t])
+            placed = {**EARLY_TILES_AT, **LATE_TILES_AT}
+            if (name, t) in placed:
+                return reused.tile([P, S], F32, name=f"{name}{t}", align_bytes=64, offset=placed[name, t])
             return keep.tile([P, S], F32, name=f"{name}{t}")
 
         score = [head_rows("score", t) for t in range(PACK)]
@@ -263,14 +265,14 @@ def tile_picked_zrandla_relu_po_kernel(
         def make_feature(t, cols, bank, copy):
             head_columns(feature[t], feature_words, feature_scales, t, cols, bank, copy)
 
-        def scratch(name):
-            return [keep.tile([P, V], F32, name=f"{name}{t}") for t in range(PACK)]
+        def scratch(name, first=0):
+            return [keep.tile([P, V], F32, name=f"{name}{t}") for t in range(first, PACK)]
 
         pooled = keep.tile([P, PACK, V], F32, align_bytes=256)
         out_rows = out_0.rearrange("(p t) v -> p t v", t=PACK)
         first_score, weight, gap = scratch("first_score"), scratch("weight"), scratch("gap")
-        base, rise, term = scratch("base"), scratch("rise"), scratch("term")
-        rise[0] = reused.tile([P, V], F32, name="first_rise", align_bytes=64, offset=FIRST_RISE_AT)
+        base, later_rises, term = scratch("base"), scratch("rise", first=1), scratch("term")
+        rise = [reused.tile([P, V], F32, name="rise0", align_bytes=64, offset=FIRST_RISE_AT)] + later_rises
         centres = slice(0, V)
         centre_halves = (slice(0, V // 2), slice(V // 2, V))
 
@@ -291,8 +293,8 @@ def tile_picked_zrandla_relu_po_kernel(
         def make_weight(t):
             nc.scalar.activation(out=weight[t][:], in_=gap[t][:], func=ACT.Sigmoid, scale=-1.0)
 
-        def fetch_base(t, part, fetch):
-            fetch(base[t][:, part], feature[t][:].indirect(entries(pos2_t, part)))
+        def fetch_base(t, part):
+            scalar_fetch(base[t][:, part], feature[t][:].indirect(entries(pos2_t, part)))
 
         def feature_rise(t, part):
             nc.vector.tensor_tensor(
@@ -302,8 +304,8 @@ def tile_picked_zrandla_relu_po_kernel(
         def weigh(t, part):
             nc.vector.tensor_tensor(term[t][:, part], rise[t][:, part], weight[t][:, part], ALU.mult)
 
-        def add_base(t, part):
-            nc.vector.tensor_tensor(pooled[:, t, part], term[t][:, part], base[t][:, part], ALU.add)
+        def add_base(t, part, engine=nc.vector):
+            engine.tensor_tensor(pooled[:, t, part], term[t][:, part], base[t][:, part], ALU.add)
 
         def store(t):
             nc.sync.dma_start(out=out_rows[:, t, :], in_=pooled[:, t, :])
@@ -329,9 +331,9 @@ def tile_picked_zrandla_relu_po_kernel(
         make_feature(1, late_points, 5, on_vector)
         fetch_first(1, centres, scalar_fetch)
         score_gap(0, centres)
-        fetch_base(0, centres, scalar_fetch)
+        fetch_base(0, centres)
         score_gap(1, centres)
-        fetch_base(1, centres, scalar_fetch)
+        fetch_base(1, centres)
         feature_rise(0, centres)
         make_weight(0)
         feature_rise(1, centres)
@@ -341,13 +343,13 @@ def tile_picked_zrandla_relu_po_kernel(
         weigh(1, centres)
         make_score(3, points, 1, on_vector)
         make_feature(3, batch_cols(3), 7, on_vector)
-        nc.gpsimd.tensor_tensor(pooled[:, 0, :], term[0][:], base[0][:], ALU.add)
+        add_base(0, centres, nc.gpsimd)
         store(0)
         make_feature(2, points, 6, on_scalar)
         fetch_first(2, centres, scalar_fetch)
         add_base(1, centres)
         store(1)
-        fetch_base(2, centres, scalar_fetch)
+        fetch_base(2, centres)
         score_gap(2, centres)
         fetch_first(3, centres, scalar_fetch)
         feature_rise(2, centres)
@@ -356,7 +358,7 @@ def tile_picked_zrandla_relu_po_kernel(
         make_weight(2)
         weigh(2, centres)
         for part in centre_halves:
-            fetch_base(3, part, scalar_fetch)
+            fetch_base(3, part)
             feature_rise(3, part)
         make_weight(3)
         round_pair(low_tiles, centres, nc.scalar.copy)

from contextlib import ExitStack

import concourse.mybir as mybir

K, T, S, V, H, N = 1024, 1024, 512, 256, 512, 512
FLOPS = 2 * S * (K * H + 2 * H * N)

F32 = mybir.dt.float32
BF16 = mybir.dt.bfloat16
I32 = mybir.dt.int32
U32 = mybir.dt.uint32
U16 = mybir.dt.uint16
U8 = mybir.dt.uint8
FP8X4 = mybir.dt.float8_e4m3fn_x4
FP4X4 = mybir.dt.float4_e2m1fn_x4
ACT = mybir.ActivationFunctionType
ALU = mybir.AluOpType

P = 128
PACK = 4
PASSES = K // (P * PACK)
BATCH = 128
BATCHES = S // BATCH
QUADRANT = 32
ROWS = 4
X_SCALES_FROM = 4
ENTRIES_PER_COLUMN = 16
QUADRANT_ORDER = (0, 2, 1, 3)
SCORES, FEATURES = 0, 1

H_SCALES_AT = 0
FEATURE_SCALES_RAW_AT = 256
VECTOR_BATCH_AT = 512
SCALAR_BATCHES_AT = 2048
SECOND_PASS_AT = 6656
EARLY_TILES_AT = {("score", 1): 512, ("feature", 0): 2560, ("feature", 1): 4608}
LATE_TILES_AT = {("score", 3): 10752, ("feature", 3): 12800}
FIRST_RISE_AT = 12288


def tile_picked_zrandla_relu_po_kernel(
    tc, x_words, x_scales, w1, w2_words, w2_scales, w3_words, w3_scales, offs, pos1, pos2, out_0, out_1, out_2
):
    nc = tc.nc
    with ExitStack() as ctx:
        lists = ctx.enter_context(tc.tile_pool(name="lists", bufs=1))
        keep = ctx.enter_context(tc.tile_pool(name="keep", bufs=1))
        reused = ctx.enter_context(tc.tile_pool(name="reused", bufs=1))
        psum = ctx.enter_context(tc.psum_pool(name="psum", bufs=1))

        head_words_raw = [
            keep.tile([P, 2 * N], U8, name="score_words_raw", align_bytes=64),
            reused.tile([P, 2 * N], U8, name="feature_words_raw", align_bytes=64, offset=SCALAR_BATCHES_AT),
        ]
        x_scale_window = keep.tile([P, T], U8, align_bytes=256)
        nc.vector.memset(x_scale_window[:].bitcast(I32), 0)
        warm = keep.tile([P, 2], F32)
        nc.vector.memset(warm[:, 0:1], 0.0)
        nc.scalar.activation(out=warm[:, 1:2], in_=warm[:, 0:1], func=ACT.Sigmoid)
        head_scales_raw = [
            keep.tile([P, N], U8, name="score_scales_raw", align_bytes=64),
            reused.tile([P, N], U8, name="feature_scales_raw", align_bytes=64, offset=FEATURE_SCALES_RAW_AT),
        ]
        nc.vector.memset(head_scales_raw[SCORES][:].bitcast(I32), 0)
        nc.vector.memset(head_scales_raw[FEATURES][:].bitcast(I32), 0)

        w1_raw = [keep.tile([P, PACK, H], F32, name=f"w1_raw{g}", align_bytes=256) for g in range(PASSES)]
        w1_rows = w1.rearrange("(g p j) c -> g p j c", p=P, j=PACK)
        x_window = [keep.tile([P, T], I32, name=f"x_window{g}", align_bytes=256) for g in range(PASSES)]
        offs_t = lists.tile([P, S // ENTRIES_PER_COLUMN], U16)
        pos1_t = lists.tile([P, V // ENTRIES_PER_COLUMN], U16)
        pos2_t = lists.tile([P, V // ENTRIES_PER_COLUMN], U16)

        def load_x(g):
            nc.sync.dma_start(out=x_window[g][:], in_=x_words[g].rearrange("p n t -> p (n t)").bitcast(I32))

        load_x(0)
        nc.sync.dma_start(offs_t[:], offs)
        for q in QUADRANT_ORDER:
            first_row = QUADRANT * q + X_SCALES_FROM
            nc.sync.dma_start(
                out=x_scale_window[first_row : first_row + ROWS * PASSES, :].bitcast(I32),
                in_=x_scales[:, ROWS * q : ROWS * q + ROWS, :].bitcast(I32),
            )

        def load_head_scales(w, scales):
            for q in QUADRANT_ORDER:
                nc.sync.dma_start(
                    out=head_scales_raw[w][QUADRANT * q : QUADRANT * q + ROWS, :].bitcast(I32),
                    in_=scales[0, ROWS * q : ROWS * q + ROWS, :].bitcast(I32),
                )

        nc.sync.dma_start(out=w1_raw[0][:], in_=w1_rows[0])
        load_head_scales(SCORES, w2_scales)
        nc.sync.dma_start(out=w1_raw[1][:], in_=w1_rows[1])
        load_x(1)
        nc.sync.dma_start(out=head_words_raw[SCORES][:].bitcast(I32), in_=w2_words[0].bitcast(I32))
        nc.sync.dma_start(out=head_words_raw[FEATURES][:].bitcast(I32), in_=w3_words[0].bitcast(I32))
        load_head_scales(FEATURES, w3_scales)
        nc.sync.dma_start(pos1_t[:], pos1)
        nc.sync.dma_start(pos2_t[:], pos2)

        def deal_words(w, dealt):
            nc.scalar.copy(
                out=dealt[:].bitcast(U16).rearrange("p (t c) -> p t c", t=PACK),
                in_=head_words_raw[w][:].bitcast(U16).rearrange("p (c t) -> p t c", t=PACK),
            )

        def deal_scales(w, dealt):
            nc.vector.tensor_copy(
                out=dealt[:].rearrange("p (t c) -> p t c", t=PACK),
                in_=head_scales_raw[w][:].rearrange("p (c t) -> p t c", t=PACK),
            )

        x_picked = [keep.tile([P, S], U32, name=f"x_picked{g}", align_bytes=64) for g in range(PASSES)]
        nc.vector.tensor_copy(x_picked[0][:], x_window[0][:].bitcast(U32).indirect(offs_t[:]))
        x_scales_picked = keep.tile([P, S], U8, align_bytes=64)
        nc.vector.tensor_copy(x_scales_picked[:], x_scale_window[:].indirect(offs_t[:]))

        w1_grouped = [
            keep.tile([P, PACK, P, PACK], BF16, name="w1_grouped0", align_bytes=64),
            reused.tile([P, PACK, P, PACK], BF16, name="w1_grouped1", align_bytes=64, offset=SECOND_PASS_AT),
        ]
        w1_codes = [keep.tile([P, H], U32, name=f"w1_codes{g}", align_bytes=64) for g in range(PASSES)]
        w1_scales = [keep.tile([P, H], U8, name=f"w1_scales{g}", align_bytes=64) for g in range(PASSES)]

        def round_w1(g, tiles, part, copy):
            copy(
                out=w1_grouped[g][:, tiles, part, :].rearrange("p t c j -> p c j t"),
                in_=w1_raw[g][:, :, PACK * part.start : PACK * part.stop].rearrange("p j (c t) -> p c j t", t=PACK)[
                    :, :, :, tiles
                ],
            )

        def quantize_w1(g, cols):
            nc.vector.quantize_mx(
                out=w1_codes[g][:, cols].bitcast(FP8X4),
                scales=w1_scales[g][:, cols],
                in_=w1_grouped[g][:].rearrange("p t c j -> p (t c j)")[:, PACK * cols.start : PACK * cols.stop],
            )

        low_tiles, high_tiles = slice(0, 2), slice(2, PACK)
        low_cols, high_cols = slice(0, 2 * P), slice(2 * P, H)
        tile_whole = slice(0, P)
        tile_halves = (slice(0, P // 2), slice(P // 2, P))
        round_w1(0, low_tiles, tile_whole, nc.scalar.copy)
        round_w1(0, high_tiles, tile_whole, nc.vector.tensor_copy)
        round_w1(1, high_tiles, tile_whole, nc.scalar.copy)

        hidden = [psum.tile([P, PACK, BATCH], F32, name=f"bank{b}") for b in range(BATCHES)]

        def entries(list_tile, part):
            return list_tile[:, part.start // ENTRIES_PER_COLUMN : part.stop // ENTRIES_PER_COLUMN]

        def batch_cols(b):
            return slice(b * BATCH, (b + 1) * BATCH)

        def pick_words(g, part):
            nc.vector.tensor_copy(x_picked[g][:, part], x_window[g][:].bitcast(U32).indirect(entries(offs_t, part)))

        h_codes = keep.tile([P, S], U32, align_bytes=64)
        h_scales = reused.tile([P, S], U8, align_bytes=64, offset=H_SCALES_AT)

        first_pass_tiles = (2, 3, 0, 1)

        def first_layer_pass(b, t, g):
            nc.tensor.matmul_mx(
                out=hidden[b][:, t, :],
                lhsT=w1_codes[g][:, t * P : (t + 1) * P].bitcast(FP8X4),
                lhsT_scale=w1_scales[g][:, t * P : (t + 1) * P],
                rhs=x_picked[g][:, batch_cols(b)].bitcast(FP8X4),
                rhs_scale=x_scales_picked[X_SCALES_FROM + ROWS * g : P, batch_cols(b)],
                start=(g == 0 and t == first_pass_tiles[0]),
                stop=(g == PASSES - 1 and t == PACK - 1),
            )

        score_scales = keep.tile([P, N], U8, align_bytes=64)
        deal_scales(SCORES, score_scales)
        quantize_w1(0, high_cols)
        quantize_w1(0, low_cols)
        for t in first_pass_tiles:
            for b in range(BATCHES):
                first_layer_pass(b, t, 0)
        for part in tile_halves:
            round_w1(1, low_tiles, part, nc.vector.tensor_copy)
        for part in tile_halves:
            for t in range(low_tiles.start, low_tiles.stop):
                quantize_w1(1, slice(t * P + part.start, t * P + part.stop))
        pick_words(1, batch_cols(0))
        quantize_w1(1, high_cols)
        for b in range(1, BATCHES):
            pick_words(1, batch_cols(b))
        score_words = keep.tile([P, 2 * N], U8, align_bytes=64)
        feature_words = keep.tile([P, 2 * N], U8, align_bytes=64)
        deal_words(SCORES, score_words)
        deal_words(FEATURES, feature_words)
        feature_scales = reused.tile([P, N], U8, align_bytes=64, offset=SECOND_PASS_AT)
        deal_scales(FEATURES, feature_scales)

        scalar_batches = reused.tile([P, BATCHES - 1, BATCH, PACK], BF16, align_bytes=64, offset=SCALAR_BATCHES_AT)
        vector_batch = reused.tile([P, BATCH, PACK], BF16, align_bytes=64, offset=VECTOR_BATCH_AT)
        h_grouped = [scalar_batches[:, b] for b in range(BATCHES - 1)] + [vector_batch[:]]
        batch_whole = slice(0, BATCH)
        batch_halves = (slice(0, BATCH // 2), slice(BATCH // 2, BATCH))

        def close_batch(b):
            for t in range(PACK):
                first_layer_pass(b, t, 1)
            return hidden[b][:].rearrange("p t e -> p e t")

        def quantize_h(b, part):
            cols = slice(b * BATCH + part.start, b * BATCH + part.stop)
            nc.vector.quantize_mx(
                out=h_codes[:, cols].bitcast(FP8X4),
                scales=h_scales[:, cols],
                in_=h_grouped[b][:, part, :].rearrange("p e t -> p (e t)"),
            )

        for b in range(2):
            nc.scalar.activation(out=h_grouped[b], in_=close_batch(b), func=ACT.Relu)
        last_sums = close_batch(2)
        for part in batch_halves:
            nc.scalar.activation(out=h_grouped[2][:, part, :], in_=last_sums[:, part, :], func=ACT.Relu)
        quantize_h(0, batch_whole)
        nc.vector.tensor_scalar_max(h_grouped[3], close_batch(3), 0.0)
        quantize_h(1, batch_whole)
        quantize_h(3, batch_whole)
        for part in batch_halves:
            quantize_h(2, part)

        def product_pieces(cols):
            if cols.stop - cols.start == 3 * BATCH:
                cut = cols.start + 2 * BATCH
                return (slice(cols.start, cut), slice(cut, cols.stop))
            return (cols,)

        def head_columns(rows, words, scales, t, cols, bank, copy):
            acc = psum.tile([P, S], F32, name=f"bank{bank}")
            for piece in product_pieces(cols):
                nc.tensor.matmul_mx(
                    out=acc[:, piece],
                    lhsT=words[:, t * 2 * P : (t + 1) * 2 * P].bitcast(FP4X4),
                    lhsT_scale=scales[:, t * P : (t + 1) * P],
                    rhs=h_codes[:, piece].bitcast(FP8X4),
                    rhs_scale=h_scales[:, piece],
                    start=True,
                    stop=True,
                )
            copy(out=rows[:, cols], in_=acc[:, cols])

        def head_rows(name, t):
            placed = {**EARLY_TILES_AT, **LATE_TILES_AT}
            if (name, t) in placed:
                return reused.tile([P, S], F32, name=f"{name}{t}", align_bytes=64, offset=placed[name, t])
            return keep.tile([P, S], F32, name=f"{name}{t}")

        score = [head_rows("score", t) for t in range(PACK)]
        feature = [head_rows("feature", t) for t in range(PACK)]

        points, early_points, late_points = slice(0, S), slice(0, S // 2), slice(S // 2, S)

        def make_score(t, cols, bank, copy):
            head_columns(score[t], score_words, score_scales, t, cols, bank, copy)

        def make_feature(t, cols, bank, copy):
            head_columns(feature[t], feature_words, feature_scales, t, cols, bank, copy)

        def scratch(name, first=0):
            return [keep.tile([P, V], F32, name=f"{name}{t}") for t in range(first, PACK)]

        pooled = keep.tile([P, PACK, V], F32, align_bytes=256)
        out_rows = out_0.rearrange("(p t) v -> p t v", t=PACK)
        first_score, weight, gap = scratch("first_score"), scratch("weight"), scratch("gap")
        base, later_rises, term = scratch("base"), scratch("rise", first=1), scratch("term")
        rise = [reused.tile([P, V], F32, name="rise0", align_bytes=64, offset=FIRST_RISE_AT)] + later_rises
        centres = slice(0, V)
        centre_halves = (slice(0, V // 2), slice(V // 2, V))

        def scalar_fetch(out, in_):
            nc.scalar.activation(out=out, in_=in_, func=ACT.Copy)

        def vector_fetch(out, in_):
            nc.vector.tensor_copy(out, in_)

        def fetch_first(t, part, fetch):
            fetch(first_score[t][:, part], score[t][:].indirect(entries(pos1_t, part)))

        def score_gap(t, part):
            nc.vector.tensor_tensor(
                gap[t][:, part], score[t][:].indirect(entries(pos2_t, part)), first_score[t][:, part], ALU.subtract
            )

        def make_weight(t):
            nc.scalar.activation(out=weight[t][:], in_=gap[t][:], func=ACT.Sigmoid, scale=-1.0)

        def fetch_base(t, part):
            scalar_fetch(base[t][:, part], feature[t][:].indirect(entries(pos2_t, part)))

        def feature_rise(t, part):
            nc.vector.tensor_tensor(
                rise[t][:, part], feature[t][:].indirect(entries(pos1_t, part)), base[t][:, part], ALU.subtract
            )

        def weigh(t, part):
            nc.vector.tensor_tensor(term[t][:, part], rise[t][:, part], weight[t][:, part], ALU.mult)

        def add_base(t, part, engine=nc.vector):
            engine.tensor_tensor(pooled[:, t, part], term[t][:, part], base[t][:, part], ALU.add)

        def store(t):
            nc.sync.dma_start(out=out_rows[:, t, :], in_=pooled[:, t, :])

        out_grouped = keep.tile([P, V, PACK], BF16, align_bytes=64)
        out_codes = keep.tile([P, V], U32, align_bytes=256)
        out_scales = keep.tile([P, V], U8, align_bytes=256)

        def round_pair(tiles, part, copy):
            copy(out=out_grouped[:, part, tiles], in_=pooled[:, tiles, part].rearrange("p t v -> p v t"))

        on_scalar, on_vector = nc.scalar.copy, nc.vector.tensor_copy
        make_score(0, batch_cols(0), 4, on_scalar)
        make_score(0, batch_cols(1), 5, on_scalar)
        make_score(0, batch_cols(3), 0, on_scalar)
        make_score(0, batch_cols(2), 4, on_scalar)
        make_score(1, early_points, 6, on_vector)
        make_feature(0, early_points, 7, on_vector)
        make_feature(1, early_points, 1, on_vector)
        make_score(1, late_points, 3, on_scalar)
        make_feature(0, late_points, 2, on_scalar)
        fetch_first(0, centres, vector_fetch)
        make_feature(1, late_points, 5, on_vector)
        fetch_first(1, centres, scalar_fetch)
        score_gap(0, centres)
        fetch_base(0, centres)
        score_gap(1, centres)
        fetch_base(1, centres)
        feature_rise(0, centres)
        make_weight(0)
        feature_rise(1, centres)
        make_weight(1)
        weigh(0, centres)
        make_score(2, points, 0, on_scalar)
        weigh(1, centres)
        make_score(3, points, 1, on_vector)
        make_feature(3, batch_cols(3), 7, on_vector)
        add_base(0, centres, nc.gpsimd)
        store(0)
        make_feature(2, points, 6, on_scalar)
        fetch_first(2, centres, scalar_fetch)
        add_base(1, centres)
        store(1)
        fetch_base(2, centres)
        score_gap(2, centres)
        fetch_first(3, centres, scalar_fetch)
        feature_rise(2, centres)
        make_feature(3, slice(0, 3 * BATCH), 4, on_scalar)
        score_gap(3, centres)
        make_weight(2)
        weigh(2, centres)
        for part in centre_halves:
            fetch_base(3, part)
            feature_rise(3, part)
        make_weight(3)
        round_pair(low_tiles, centres, nc.scalar.copy)
        for part in centre_halves:
            weigh(3, part)
            add_base(2, part)
        store(2)
        for part in centre_halves:
            add_base(3, part)
        store(3)

        for part in centre_halves:
            round_pair(high_tiles, part, nc.vector.tensor_copy)
        for part in centre_halves:
            nc.vector.quantize_mx(
                out=out_codes[:, part].bitcast(FP8X4),
                scales=out_scales[:, part],
                in_=out_grouped[:, part, :].rearrange("p v t -> p (v t)"),
            )
        nc.sync.dma_start(out=out_1[0].rearrange("p c r -> p (c r)").bitcast(I32), in_=out_codes[:].bitcast(I32))
        for q, queue in enumerate((nc.sync, nc.sync, nc.sync, nc.scalar)):
            queue.dma_start(
                out=out_2[0, ROWS * q : ROWS * q + ROWS, :].bitcast(I32),
                in_=out_scales[QUADRANT * q : QUADRANT * q + ROWS, :].bitcast(I32),
            )
